import numpy as np, ml_dtypes
CORES = [24,25,26,27,28,29,30,31,224,225,226,227,228,229,230,231]
N = 16
S, T = 16384, 2048
def entries(a): return a.T.reshape(-1)
def pack(v, P): return np.ascontiguousarray(np.asarray(v, np.int32).reshape(-1, P).T)
def lists(rng, how):
    M = rng.integers(0, S, (N, S)); b = rng.integers(0, S, T)
    if how == "alike": M = np.stack([rng.permutation(S) for f in range(N)]); b[:] = rng.integers(S)
    if how == "edge":
        M = np.where(rng.random((N, S)) < 0.5, 0, S - 1); w = rng.permutation(N) % 2 * (S - 1); M[:, 0] = w; M[:, S - 1] = S - 1 - w
        b = np.where(rng.random(T) < 0.5, 0, S - 1); b[rng.permutation(T)[:2]] = [0, S - 1]
    if how == "fold":
        V = np.stack([rng.permutation(S)[:4] for f in range(N + 1)]); M = V[np.arange(N)[:, None], rng.integers(0, 4, (N, S))]
        M[np.arange(N)[:, None], V[1:]] = V[:N]; b[rng.permutation(T)[:4]] = V[N]
    if how == "mixed":
        k = np.concatenate([[3, 3], rng.permutation(np.arange(N - 2) % 3)])
        for f in range(N): M[f] = [np.arange(S), rng.permutation(S), M[f], rng.integers(0, S, 4)[rng.integers(0, 4, S)]][k[f]]
    if how == "turn": M = np.stack([rng.permutation(S) for f in range(N)]); b = rng.permutation(S)[:T]
    return {"bp": np.stack([pack(m, 16) for m in M]), "st": np.broadcast_to(pack(b, 16), (N, 16, T // 16)).copy()}
def setup_inputs(rng):
    return dict({"tab": rng.standard_normal((N, 128, S), dtype=np.float32).astype(ml_dtypes.bfloat16)}, **lists(rng, "uniform"))
def setup_inputs_alike(rng):
    d = setup_inputs(rng); d.update(lists(rng, "alike"))
    for k in ("tab",): d[k] = (d[k].astype(np.float32) * 1048576.0).astype(d[k].dtype)
    return d
def setup_inputs_edge(rng):
    d = setup_inputs(rng); d.update(lists(rng, "edge"))
    for k in ("tab",): d[k] = (d[k].astype(np.float32) * (1 / 1024.0)).astype(d[k].dtype)
    return d
def setup_inputs_fold(rng):
    d = setup_inputs(rng); d.update(lists(rng, "fold"))
    return d
def setup_inputs_mixed(rng):
    d = setup_inputs(rng); d.update(lists(rng, "mixed"))
    return d
def setup_inputs_turn(rng):
    d = setup_inputs(rng); d.update(lists(rng, "turn"))
    return d
def check_inputs(x):
    bad = []
    if x["bp"].min() < 0 or x["bp"].max() >= S: bad.append("bp out of range")
    if x["st"].min() < 0 or x["st"].max() >= S: bad.append("st out of range")
    if not all(np.array_equal(a, x["st"][0]) for a in x["st"]): bad.append("st isn't alike on all ranks")
    return bad
def reference(tab, bp, st):
    b = entries(st[0]); y = np.zeros((N, 128, T), tab.dtype)
    for f in range(N - 1, -1, -1):
        y[f] = tab[f][:, b]
        b = entries(bp[f])[b]
    return {"y": y}

@@ -1,0 +1,437 @@
+from concourse.bass import DstId, RemoteDMATransfer
+from concourse.mybir import AluOpType, ActivationFunctionType
+
+N = 16
+CH = 1024
+NCH = 16384 // CH
+HOPS = N - 1
+BATCHES = [[14, 13, 12, 11], [10, 9, 8], [7, 6, 5, 4], [3, 2, 1], [0]]
+
+SCRATCH = {
+    "tabs": ("sbuf", [128, 16384], "bfloat16"),
+    "yt": ("sbuf", [128, 2048], "bfloat16"),
+    "maps": ("sbuf", [128, 256 * N], "bfloat16"),
+    "bpi": ("sbuf", [128, 128], "int32"),
+    "i1": ("sbuf", [128, 128], "int32"),
+    "i2": ("sbuf", [128, 128], "int32"),
+    "i3": ("sbuf", [128, 128], "int32"),
+    "i4": ("sbuf", [128, 128], "int32"),
+    "kd": ("sbuf", [128, 128], "bfloat16"),
+    "md": ("sbuf", [128, 128], "bfloat16"),
+    "dmat": ("sbuf", [128, 128], "bfloat16"),
+    "ident": ("sbuf", [128, 128], "bfloat16"),
+    "ones": ("sbuf", [128, 128], "bfloat16"),
+    "w1": ("sbuf", [128, 128], "bfloat16"),
+    "w2": ("sbuf", [128, 128], "bfloat16"),
+    "w3": ("sbuf", [128, 128], "bfloat16"),
+    "pcol": ("sbuf", [128, 4], "float32"),
+    "bcol": ("sbuf", [128, 4], "float32"),
+    "stc": ("sbuf", [128, 2], "int32"),
+    "s1": ("sbuf", [128, 2], "int32"),
+    "s2": ("sbuf", [128, 2], "int32"),
+    "s3": ("sbuf", [128, 2], "int32"),
+    "s4": ("sbuf", [128, 2], "int32"),
+    "d0": ("sbuf", [128, 4], "float32"),
+    "z": ("sbuf", [128, 512], "bfloat16"),
+    "stf": ("sbuf", [128, 128], "int32"),
+    "th0": ("sbuf", [128, 256], "bfloat16"),
+    "th1": ("sbuf", [128, 256], "bfloat16"),
+    "ol0": ("sbuf", [128, 256], "bfloat16"),
+    "ol1": ("sbuf", [128, 256], "bfloat16"),
+    "bk0": ("sbuf", [128, 256], "bfloat16"),
+    "bk1": ("sbuf", [128, 256], "bfloat16"),
+    "bm0": ("sbuf", [128, 256], "bfloat16"),
+    "bm1": ("sbuf", [128, 256], "bfloat16"),
+    "dd": ("sbuf", [128, 8 * N], "float32"),
+    "colall": ("sbuf", [128, 32], "float32"),
+    "du1": ("sbuf", [128, 8], "int32"),
+    "du2": ("sbuf", [128, 8], "int32"),
+    "dur": ("sbuf", [128, 8], "uint16"),
+    "duk": ("sbuf", [128, 16], "uint16"),
+    "ri": ("sbuf", [128, 16], "int32"),
+    "ltr": ("sbuf", [128, 128], "bfloat16"),
+    "ltk": ("sbuf", [128, 256], "bfloat16"),
+    "off": ("sbuf", [128, 128], "uint16"),
+    "pak0": ("psum", [128, 512], "float32"),
+    "pak1": ("psum", [128, 512], "float32"),
+    "pam0": ("psum", [128, 512], "float32"),
+    "pam1": ("psum", [128, 512], "float32"),
+    "pck0": ("psum", [128, 512], "float32"),
+    "pck1": ("psum", [128, 512], "float32"),
+    "pcm0": ("psum", [128, 512], "float32"),
+    "pcm1": ("psum", [128, 512], "float32"),
+}
+SEMAPHORES = (["bpld", "stld", "stfl", "tab", "yst", "msd", "msi", "mso", "gq", "gdm", "gid", "gpb", "gdu", "dv", "dkd",
+               "dmd", "pdk", "pdm", "mk", "mm", "zz", "wi", "duo", "bsent", "fsent", "sent", "esent", "col", "rr", "lr",
+               "lk", "po", "of", "yv0", "yv1", "ya0", "ya1"]
+              + ["map%d" % f for f in range(1, N)] + ["rel%d" % k for k in range(len(BATCHES))]
+              + [n + x for x in "01" for n in ("th", "ol", "ak", "am", "bk", "bm", "ck", "cm", "ev")])
+
+
+def _bits(mask):
+    return [b for b in range(16) if mask >> b & 1]
+
+
+def _mask(bits):
+    return sum(1 << b for b in bits)
+
+
+def rank_program(g, core, T, topo):
+    R = T.rank_of(core)
+    if R is None:
+        return
+    A, F, S = AluOpType, ActivationFunctionType, T.sem
+    cores = list(T.cores)
+    place = lambda c: (topo.host(c), topo.chip(c))
+    front = [f for f in range(N) if place(cores[f]) == place(cores[N - 1])]
+    back = [f for f in range(N) if f not in front]
+
+    def pair_up(own, far):
+        out = []
+        for d in sorted(set(topo.die(cores[f]) for f in own)):
+            on = [f for f in own if topo.die(cores[f]) == d]
+            ports = [f for f in on if topo.may_write(cores[f], cores[far])]
+            rest = [f for f in on if f not in ports]
+            out += list(zip(ports, rest))
+        return out
+    fpairs, bpairs = pair_up(front, back[0]), pair_up(back, front[0])
+    slot = {}
+    for u, (p, n) in enumerate(fpairs):
+        slot[p], slot[n] = 2 * u, 2 * u + 1
+    lander = {f: front[i] for i, f in enumerate(back)}
+    is_front = R in front
+
+    def bits(dst):
+        return _bits(topo.mask(core, cores[dst]))
+
+    def ident_of(dst):
+        rid, pid = topo.addr(cores[dst], core)
+        return DstId(rid=rid, pnc=pid)
+
+    def xfer(dsts, src, dst_ap, sem, eng):
+        return RemoteDMATransfer(dst_ids=[ident_of(d) for d in dsts], dma_engine_mask=_mask(eng), remote_sem=sem,
+                                 srcs=[src], dsts=[dst_ap for _ in dsts])
+
+    def mapslot(f):
+        return T.maps[:, 256 * f:256 * f + 256]
+
+    def par(t, h):
+        return t[:, 128 * (h % 2):128 * (h % 2) + 128]
+    TH, OL, BK, BM = [T.th0, T.th1], [T.ol0, T.ol1], [T.bk0, T.bk1], [T.bm0, T.bm1]
+    PAK, PAM, PCK, PCM = [T.pak0, T.pak1], [T.pam0, T.pam1], [T.pck0, T.pck1], [T.pcm0, T.pcm1]
+    has_map = R >= 1
+    from_st = R == N - 1
+
+    done = [0]
+
+    def load_tab(n):
+        for _ in range(n):
+            a = done[0] * CH
+            g.sync.dma_start(T.tabs[:, a:a + CH], T.tab[:, a:a + CH]).then_inc(S.tab, 16)
+            done[0] += 1
+    if has_map:
+        g.sync.dma_start(T.bpi[:, :], T.bp[:, :]).then_inc(S.bpld, 16)
+
+    if is_front:
+        for x in (0, 1):
+            t = 2 * slot[R] + x
+            g.scalar.dma_start(T.stc[:, x:x + 1], T.st[t:t + 1, :]).then_inc(S.stld, 16)
+    if from_st:
+        for q in range(8):
+            g.scalar.dma_start(T.stf[16 * q:16 * q + 16, :], T.st[:, :]).then_inc(S.stfl, 16)
+
+    v = g.vector
+    if has_map:
+        v.memset(T.dmat[:, :], 0.0).then_inc(S.msd, 1)
+    v.memset(T.ident[:, :], 0.0).then_inc(S.msi, 1)
+    if is_front:
+        v.memset(T.ones[:, :], 1.0).then_inc(S.mso, 1)
+    if has_map:
+        g.wait_ge(S.msd, 1)
+        g.affine_select(T.dmat[:, :], T.dmat[:, :], [[-1, 128]], A.not_equal, 0.5, 0, 1).then_inc(S.gq, 1)
+        g.wait_ge(S.gq, 1)
+        g.affine_select(T.dmat[:, :], T.dmat[:, :], [[1, 128]], A.not_equal, -0.5, -1, -1).then_inc(S.gq, 1)
+        g.wait_ge(S.gq, 2)
+        g.affine_select(T.dmat[:, :], T.dmat[:, :], [[-1, 128]], A.not_equal, 0.5, -127, 1).then_inc(S.gdm, 1)
+    g.wait_ge(S.msi, 1)
+    g.affine_select(T.ident[:, :], T.ident[:, :], [[-1, 128]], A.not_equal, 1.0, 0, 1).then_inc(S.gid, 1)
+    if is_front:
+        g.iota(T.pcol[:, 0:1], [[1, 1]], 0, 1, allow_small_or_imprecise_dtypes=True).then_inc(S.gpb, 1)
+        g.iota(T.bcol[:, 0:1], [[1, 1]], 1, -2, allow_small_or_imprecise_dtypes=True).then_inc(S.gpb, 1)
+    if not from_st:
+        g.iota(T.du1[:, :], [[0, 8]], 0, 1).then_inc(S.gdu, 1)
+
+    dv = [0]
+
+    def inc(op):
+        op.then_inc(S.dv, 1)
+        dv[0] += 1
+
+    def dvw():
+        v.wait_ge(S.dv, dv[0])
+    if has_map:
+        v.wait_ge(S.bpld, 16)
+        inc(v.tensor_scalar(T.i1[:, :], T.bpi[:, :], 15, None, A.bitwise_and))
+        inc(v.tensor_scalar(T.i2[:, :], T.bpi[:, :], 11, None, A.arith_shift_right))
+        dvw()
+        inc(v.tensor_scalar(T.i3[:, :], T.i1[:, :], 8, None, A.mult))
+        inc(v.tensor_scalar(T.i4[:, :], T.bpi[:, :], 4, 127, A.arith_shift_right, A.bitwise_and))
+        dvw()
+        v.tensor_tensor(T.kd[:, :], T.i3[:, :], T.i2[:, :], A.add).then_inc(S.dkd, 1)
+        v.tensor_copy(T.md[:, :], T.i4[:, :]).then_inc(S.dmd, 1)
+        g.tensor.wait_ge(S.gdm, 1)
+        g.tensor.wait_ge(S.dkd, 1)
+        g.tensor.matmul(T.pak0[:, 0:128], T.dmat[:, :], T.kd[:, :], True, True).then_inc(S.pdk, 1)
+        g.tensor.wait_ge(S.dmd, 1)
+        g.tensor.matmul(T.pam0[:, 0:128], T.dmat[:, :], T.md[:, :], True, True).then_inc(S.pdm, 1)
+        v.wait_ge(S.pdk, 1)
+        v.tensor_copy(T.maps[:, 256 * R:256 * R + 128], T.pak0[:, 0:128]).then_inc(S.mk, 1)
+        g.scalar.wait_ge(S.pdm, 1)
+        g.scalar.activation(T.maps[:, 256 * R + 128:256 * R + 256], T.pam0[:, 0:128], F.Copy).then_inc(S.mm, 1)
+    if not from_st:
+        g.scalar.wait_ge(S.gid, 1)
+        for t, w in ((T.w1, 2048.0), (T.w2, 16.0), (T.w3, -16384.0)):
+            g.scalar.activation(t[:, :], T.ident[:, :], F.Copy, scale=w).then_inc(S.wi, 1)
+
+    def repeat_offsets():
+        v.wait_ge(S.gdu, 1)
+        inc(v.tensor_scalar(T.du2[:, :], T.du1[:, :], 15, None, A.bitwise_and))
+        dvw()
+        v.tensor_copy(T.dur[:, :], T.du2[:, :]).then_inc(S.duo, 1)
+        v.tensor_scalar(T.duk[:, 0:8], T.du2[:, :], 2, None, A.mult).then_inc(S.duo, 1)
+        v.tensor_scalar(T.duk[:, 8:16], T.du2[:, :], 2, 1, A.mult, A.add).then_inc(S.duo, 1)
+    if is_front:
+        v.wait_ge(S.stld, 32)
+        inc(v.tensor_scalar(T.s1[:, :], T.stc[:, :], 15, None, A.bitwise_and))
+        inc(v.tensor_scalar(T.s2[:, :], T.stc[:, :], 11, None, A.arith_shift_right))
+        inc(v.tensor_scalar(T.s4[:, :], T.stc[:, :], 4, 127, A.arith_shift_right, A.bitwise_and))
+        dvw()
+        inc(v.tensor_scalar(T.s3[:, :], T.s1[:, :], 8, None, A.mult))
+        inc(v.tensor_copy(T.d0[:, 2:4], T.s4[:, :]))
+        dvw()
+        inc(v.tensor_tensor(T.d0[:, 0:2], T.s3[:, :], T.s2[:, :], A.add))
+        dvw()
+        v.wait_ge(S.gid, 1)
+        for j in range(4):
+            v.tensor_scalar(T.z[:, 128 * j:128 * j + 128], T.ident[:, :], T.d0[:, j:j + 1], None,
+                            A.mult).then_inc(S.zz, 1)
+        te = g.tensor
+        te.wait_ge(S.mso, 1)
+        te.wait_ge(S.zz, 4)
+        te.wait_ge(S.mk, 1)
+        te.wait_ge(S.mm, 1)
+        for x in (0, 1):
+            te.matmul(PCK[x][:, 0:128], T.ones[:, :], T.z[:, 128 * x:128 * x + 128], True, True).then_inc(S["ck%d" % x], 1)
+            te.matmul(PCM[x][:, 0:128], T.ones[:, :], T.z[:, 256 + 128 * x:384 + 128 * x], True,
+                      True).then_inc(S["cm%d" % x], 1)
+        v.wait_ge(S.gpb, 2)
+        g.scalar.wait_ge(S.gpb, 2)
+        if from_st:
+            v.wait_ge(S.stfl, 128)
+            v.tensor_copy(T.off[:, :], T.stf[:, :]).then_inc(S.of, 1)
+    if not from_st:
+        repeat_offsets()
+
+    if is_front:
+        me = slot[R]
+
+        def code(x, h):
+            g.scalar.wait_ge(S["ck%d" % x], h + 1)
+            g.scalar.activation(par(TH[x], h), PCK[x][:, 0:128], F.Sign, bias=T.bcol[:, 0:1],
+                                scale=2.0).then_inc(S["th%d" % x], 1)
+            v.wait_ge(S["cm%d" % x], h + 1)
+            v.tensor_scalar(par(OL[x], h), PCM[x][:, 0:128], T.pcol[:, 0:1], None,
+                            A.is_equal).then_inc(S["ol%d" % x], 1)
+
+        def evac(x, h):
+            f = HOPS - 1 - h
+            out = T.colall[:, 4 * me + 2 * x:4 * me + 2 * x + 2] if f == R else T.dd[:, 8 * f + 2 * x:8 * f + 2 * x + 2]
+            v.wait_ge(S["cm%d" % x], h + 2)
+            v.tensor_copy(out, PCM[x][:, 128:130]).then_inc(S["ev%d" % x], 1)
+
+        def rows(x, h):
+            f = N - 1 - h
+            te.wait_ge(S["th%d" % x], h + 1)
+            if x == 0 and f != R:
+                if f in front:
+                    n = len(bits(f))
+                elif lander[f] == R:
+                    n = len(_bits(topo.mask(cores[back[0]], core) or topo.mask(core, cores[back[0]]) or
+                                  topo.mask(cores[bpairs[0][0]], core)))
+                else:
+                    n = len(bits(lander[f]))
+                te.wait_ge(S["map%d" % f], n)
+            te.matmul(PAK[x][:, 0:128], T.maps[:, 256 * f:256 * f + 128], par(TH[x], h), True,
+                      True).then_inc(S["ak%d" % x], 1)
+            te.matmul(PAM[x][:, 0:128], T.maps[:, 256 * f + 128:256 * f + 256], par(TH[x], h), True,
+                      True).then_inc(S["am%d" % x], 1)
+
+        def pick(x, h):
+            v.wait_ge(S["ol%d" % x], h + 1)
+            v.wait_ge(S["ak%d" % x], h + 1)
+            v.tensor_tensor(par(BK[x], h), PAK[x][:, 0:128], par(OL[x], h), A.mult).then_inc(S["bk%d" % x], 1)
+            v.wait_ge(S["am%d" % x], h + 1)
+            v.tensor_tensor(par(BM[x], h), PAM[x][:, 0:128], par(OL[x], h), A.mult).then_inc(S["bm%d" % x], 1)
+
+        def sums(x, h):
+            last = h == HOPS - 1
+            te.wait_ge(S["bk%d" % x], h + 1)
+            if not last:
+                te.matmul(PCK[x][:, 0:128], T.ones[:, :], par(BK[x], h), True, True).then_inc(S["ck%d" % x], 1)
+            te.wait_ge(S["bm%d" % x], h + 1)
+            if h:
+                te.wait_ge(S["ev%d" % x], h)
+            if not last:
+                te.matmul(PCM[x][:, 0:128], T.ones[:, :], par(BM[x], h), True, True)
+            te.matmul(PCM[x][:, 128:129], par(BK[x], h), T.ones[:, 0:1], True, True)
+            te.matmul(PCM[x][:, 129:130], par(BM[x], h), T.ones[:, 0:1], True, True).then_inc(S["cm%d" % x], 1)
+
+        code(0, 0)
+        code(1, 0)
+        for h in range(HOPS):
+            rows(0, h)
+            pick(0, h)
+            if h:
+                sums(1, h - 1)
+                code(1, h)
+                evac(1, h - 1)
+            rows(1, h)
+            pick(1, h)
+            sums(0, h)
+            if h < HOPS - 1:
+                code(0, h + 1)
+            evac(0, h)
+        sums(1, HOPS - 1)
+        evac(1, HOPS - 1)
+
+    nsent = [0]
+    relay_map = None
+    if has_map:
+        g.wait_ge(S.mk, 1)
+        g.wait_ge(S.mm, 1)
+    if is_front:
+        peers = [front[(front.index(R) + k) % len(front)] for k in range(1, len(front))]
+        eng = bits(peers[0])
+        g.remote_dma_fused([xfer(peers, mapslot(R), mapslot(R), S["map%d" % R], eng)], local_sem=S.bsent)
+        nb = len(eng)
+        landed = [f for f in back if lander[f] == R and f >= 1]
+        for f in landed:
+            src = [p for p, n in bpairs if f in (p, n)][0]
+            g.wait_ge(S["map%d" % f], len(_bits(topo.mask(cores[src], core))))
+            g.remote_dma_fused([xfer(peers, mapslot(f), mapslot(f), S["map%d" % f], eng)], local_sem=S.sent)
+            nsent[0] += nb
+        port = [p for p, n in fpairs if R in (p, n)][0]
+        mate = [n for p, n in fpairs if p == port][0]
+        ne = 0
+        for k, fs in enumerate(BATCHES):
+            urgent = fs == [0]
+            to_front = fs[0] in front
+            todo = [f for f in fs if f != R]
+            g.wait_ge(S.ev0, HOPS - fs[-1])
+            g.wait_ge(S.ev1, HOPS - fs[-1])
+            if to_front:
+                dst, w = (lambda f: f), 4
+                out = T.colall[:, 4 * me:4 * me + 4]
+            elif R == port:
+                inb = _bits(topo.mask(cores[mate], core))
+                per = len(inb) if urgent else len(inb) // 4
+                g.wait_ge(S["rel%d" % k], per * len(fs))
+                dst, w = (lambda f: f), 8
+                out = T.colall[:, 4 * me:4 * me + 8]
+            else:
+                dst, w = (lambda f: port), 4
+                out = None
+            trs = []
+            for j, f in enumerate(todo):
+                e = bits(dst(f))
+                if not urgent:
+                    q = len(e) // 4
+                    e = e[q * j:q * j + q]
+                o = out if out is not None else T.dd[:, 8 * f + 4:8 * f + 8]
+                sem = S["rel%d" % k] if out is None else S.col
+                trs.append(xfer([dst(f)], T.dd[:, 8 * f:8 * f + w], o, sem, e))
+                if urgent:
+                    ne = len(e)
+                else:
+                    nsent[0] += len(e)
+            g.remote_dma_fused(trs, local_sem=S.esent if urgent else S.sent)
+    elif has_map:
+        port = [p for p, n in bpairs if R in (p, n)][0]
+        mate = [n for p, n in bpairs if p == port][0]
+        to = lander[R] if R == port else port
+        e = bits(to)
+        g.remote_dma_fused([xfer([to], mapslot(R), mapslot(R), S["map%d" % R], e)], local_sem=S.bsent)
+        nb = len(e)
+        if R == port and mate >= 1:
+            relay_map = mate
+            g.wait_ge(S["map%d" % mate], len(_bits(topo.mask(cores[mate], core))))
+            e = bits(lander[mate])
+            g.remote_dma_fused([xfer([lander[mate]], mapslot(mate), mapslot(mate), S["map%d" % mate], e)],
+                               local_sem=S.fsent)
+            nf = len(e)
+
+    if is_front:
+        if not from_st:
+            load_tab(1)
+        g.sync.wait_ge(S.bsent, nb)
+        load_tab(3)
+        for h in range(9):
+            g.sync.wait_ge(S.ev0, h + 1)
+            load_tab(1)
+        g.sync.wait_ge(S.esent, ne)
+        load_tab(NCH - done[0])
+        if nsent[0]:
+            g.wait_ge(S.sent, nsent[0])
+    elif has_map:
+        load_tab(2)
+        g.sync.wait_ge(S.bsent, nb)
+        if relay_map is not None:
+            load_tab(3)
+            g.sync.wait_ge(S.fsent, nf)
+        load_tab(NCH - done[0])
+    else:
+        load_tab(NCH)
+
+    if not from_st:
+        if is_front:
+            total = (len(front) - 1) * (len(bits(peers[0])) // 4)
+        else:
+            per = len(_bits(topo.mask(cores[fpairs[0][0]], core)))
+            total = len(fpairs) * (per if R == 0 else per // 4)
+        for q in (v, g.scalar):
+            q.wait_ge(S.col, total)
+            if is_front:
+                q.wait_ge(S.ev0, HOPS)
+                q.wait_ge(S.ev1, HOPS)
+            q.wait_ge(S.duo, 3)
+        v.tensor_scalar(T.ri[:, :], T.colall[:, 0:32:2], 0.125, -0.4375, A.mult, A.add).then_inc(S.rr, 1)
+        v.wait_ge(S.rr, 1)
+        v.tensor_copy(T.ltr[:, :], T.ri[:, 0:16].indirect(T.dur[:, 0:8])).then_inc(S.lr, 1)
+        g.scalar.activation(T.ltk[:, :], T.colall[:, 0:32].indirect(T.duk[:, 0:16]), F.Copy).then_inc(S.lk, 1)
+        te = g.tensor
+        te.wait_ge(S.wi, 3)
+        te.wait_ge(S.gid, 1)
+        te.wait_ge(S.lr, 1)
+        po = T.pck0[:, 0:128]
+        te.matmul(po, T.ltr[:, :], T.w3[:, :], True, False)
+        te.matmul(po, T.ltr[:, :], T.ident[:, :], False, False)
+        te.wait_ge(S.lk, 1)
+        te.matmul(po, T.ltk[:, 0:128], T.w1[:, :], False, False)
+        te.matmul(po, T.ltk[:, 128:256], T.w2[:, :], False, True).then_inc(S.po, 1)
+        v.wait_ge(S.po, 1)
+        v.tensor_copy(T.off[:, :], po).then_inc(S.of, 1)
+
+    for q, base, names in ((v, 0, ("yv0", "yv1")), (g.scalar, 1024, ("ya0", "ya1"))):
+        q.wait_ge(S.of, 1)
+        q.wait_ge(S.tab, 16 * NCH)
+        for k, nm in enumerate(names):
+            a = base + 512 * k
+            src = T.tabs[:, 0:16384].indirect(T.off[:, a // 16:a // 16 + 32])
+            if base:
+                q.activation(T.yt[:, a:a + 512], src, F.Copy).then_inc(S[nm], 1)
+            else:
+                q.tensor_copy(T.yt[:, a:a + 512], src).then_inc(S[nm], 1)
+    for a, nm in ((0, "yv0"), (1024, "ya0"), (512, "yv1"), (1536, "ya1")):
+        g.sync.wait_ge(S[nm], 1)
+        g.sync.dma_start(T.y[:, a:a + 512], T.yt[:, a:a + 512]).then_inc(S.yst, 16)
+    g.sync.wait_ge(S.yst, 64)

@@ -2,78 +2,30 @@ from concourse.bass import DstId, RemoteDMATransfer
 from concourse.mybir import AluOpType, ActivationFunctionType
 
 N = 16
-CH = 1024
+CH = 2048
 NCH = 16384 // CH
 HOPS = N - 1
 BATCHES = [[14, 13, 12, 11], [10, 9, 8], [7, 6, 5, 4], [3, 2, 1], [0]]
+TAB_AT = (1, 3, 5, 7)
 
-SCRATCH = {
-    "tabs": ("sbuf", [128, 16384], "bfloat16"),
-    "yt": ("sbuf", [128, 2048], "bfloat16"),
-    "maps": ("sbuf", [128, 256 * N], "bfloat16"),
-    "bpi": ("sbuf", [128, 128], "int32"),
-    "i1": ("sbuf", [128, 128], "int32"),
-    "i2": ("sbuf", [128, 128], "int32"),
-    "i3": ("sbuf", [128, 128], "int32"),
-    "i4": ("sbuf", [128, 128], "int32"),
-    "kd": ("sbuf", [128, 128], "bfloat16"),
-    "md": ("sbuf", [128, 128], "bfloat16"),
-    "dmat": ("sbuf", [128, 128], "bfloat16"),
-    "ident": ("sbuf", [128, 128], "bfloat16"),
-    "ones": ("sbuf", [128, 128], "bfloat16"),
-    "w1": ("sbuf", [128, 128], "bfloat16"),
-    "w2": ("sbuf", [128, 128], "bfloat16"),
-    "w3": ("sbuf", [128, 128], "bfloat16"),
-    "pcol": ("sbuf", [128, 4], "float32"),
-    "bcol": ("sbuf", [128, 4], "float32"),
-    "stc": ("sbuf", [128, 2], "int32"),
-    "s1": ("sbuf", [128, 2], "int32"),
-    "s2": ("sbuf", [128, 2], "int32"),
-    "s3": ("sbuf", [128, 2], "int32"),
-    "s4": ("sbuf", [128, 2], "int32"),
-    "d0": ("sbuf", [128, 4], "float32"),
-    "z": ("sbuf", [128, 512], "bfloat16"),
-    "stf": ("sbuf", [128, 128], "int32"),
-    "th0": ("sbuf", [128, 256], "bfloat16"),
-    "th1": ("sbuf", [128, 256], "bfloat16"),
-    "ol0": ("sbuf", [128, 256], "bfloat16"),
-    "ol1": ("sbuf", [128, 256], "bfloat16"),
-    "bk0": ("sbuf", [128, 256], "bfloat16"),
-    "bk1": ("sbuf", [128, 256], "bfloat16"),
-    "bm0": ("sbuf", [128, 256], "bfloat16"),
-    "bm1": ("sbuf", [128, 256], "bfloat16"),
-    "dd": ("sbuf", [128, 8 * N], "float32"),
-    "colall": ("sbuf", [128, 32], "float32"),
-    "du1": ("sbuf", [128, 8], "int32"),
-    "du2": ("sbuf", [128, 8], "int32"),
-    "dur": ("sbuf", [128, 8], "uint16"),
-    "duk": ("sbuf", [128, 16], "uint16"),
-    "ri": ("sbuf", [128, 16], "int32"),
-    "ltr": ("sbuf", [128, 128], "bfloat16"),
-    "ltk": ("sbuf", [128, 256], "bfloat16"),
-    "off": ("sbuf", [128, 128], "uint16"),
-    "pak0": ("psum", [128, 512], "float32"),
-    "pak1": ("psum", [128, 512], "float32"),
-    "pam0": ("psum", [128, 512], "float32"),
-    "pam1": ("psum", [128, 512], "float32"),
-    "pck0": ("psum", [128, 512], "float32"),
-    "pck1": ("psum", [128, 512], "float32"),
-    "pcm0": ("psum", [128, 512], "float32"),
-    "pcm1": ("psum", [128, 512], "float32"),
-}
-SEMAPHORES = (["bpld", "stld", "stfl", "tab", "yst", "msd", "msi", "mso", "gq", "gdm", "gid", "gpb", "gdu", "dv", "dkd",
-               "dmd", "pdk", "pdm", "mk", "mm", "zz", "wi", "duo", "bsent", "fsent", "sent", "esent", "col", "rr", "lr",
-               "lk", "po", "of", "yv0", "yv1", "ya0", "ya1"]
-              + ["map%d" % f for f in range(1, N)] + ["rel%d" % k for k in range(len(BATCHES))]
-              + [n + x for x in "01" for n in ("th", "ol", "ak", "am", "bk", "bm", "ck", "cm", "ev")])
+SCRATCH = {}
+for _dt, _names in (("bfloat16", "tabs:16384 yt:2048 maps:4096 kd:128 md:128 dmat:128 ident:128 ones:128 w1:128 w2:128 "
+                                 "z:256 th:256 ol:256 bk:256 bm:256 ltc:128 ltk:256"),
+                    ("int32", "bpi:128 i1:128 i2:128 i4:128 stc:1 s1:1 s2:1 s4:1 stf:128 pi:8 p1:8 p2:8 p3:8 p4:8 p5:8 "
+                              "ci:16"),
+                    ("float32", "pcol:4 bcol:4 d0:2 dd:128 colall:64"),
+                    ("uint16", "duc:8 duk:16 off:128")):
+    for _e in _names.split():
+        SCRATCH[_e.split(":")[0]] = ("sbuf", [128, int(_e.split(":")[1])], _dt)
+for _e in ("pak", "pam", "pck", "pcm", "pr0", "pr1", "pof"):
+    SCRATCH[_e] = ("psum", [128, 512], "float32")
+SEMAPHORES = ("bpld stld stfl tab yst msd msi mso gq gdm gid gpc gpi bco dv dkd dmd pdk pdm mk mm zz wi duo bsent lsent "
+              "sent esent col th ol ak am bk bm ck cm cr ev rr lc lk po of yv0 yv1 ya0 ya1").split()
+SEMAPHORES += ["map%d" % f for f in range(1, N)] + ["rel%d" % k for k in range(len(BATCHES))]
 
 
 def _bits(mask):
     return [b for b in range(16) if mask >> b & 1]
-
-
-def _mask(bits):
-    return sum(1 << b for b in bits)
 
 
 def rank_program(g, core, T, topo):
@@ -81,86 +33,81 @@ def rank_program(g, core, T, topo):
     if R is None:
         return
     A, F, S = AluOpType, ActivationFunctionType, T.sem
+    v, te, sc, sy = g.vector, g.tensor, g.scalar, g.sync
     cores = list(T.cores)
-    place = lambda c: (topo.host(c), topo.chip(c))
-    front = [f for f in range(N) if place(cores[f]) == place(cores[N - 1])]
-    back = [f for f in range(N) if f not in front]
+    place = lambda f: (topo.host(cores[f]), topo.chip(cores[f]))
+    mine = [f for f in range(N) if place(f) == place(R)]
+    other = [f for f in range(N) if f not in mine]
 
     def pair_up(own, far):
         out = []
         for d in sorted(set(topo.die(cores[f]) for f in own)):
             on = [f for f in own if topo.die(cores[f]) == d]
             ports = [f for f in on if topo.may_write(cores[f], cores[far])]
-            rest = [f for f in on if f not in ports]
-            out += list(zip(ports, rest))
+            out += list(zip(ports, [f for f in on if f not in ports]))
         return out
-    fpairs, bpairs = pair_up(front, back[0]), pair_up(back, front[0])
-    slot = {}
-    for u, (p, n) in enumerate(fpairs):
-        slot[p], slot[n] = 2 * u, 2 * u + 1
-    lander = {f: front[i] for i, f in enumerate(back)}
-    is_front = R in front
+    pairs = {f: pair_up(own, far[0]) for own, far in ((mine, other), (other, mine)) for f in own}
+    port = {f: [p for p, n in pairs[f] if f in (p, n)][0] for f in range(N)}
+    partner = {f: [n + p - f for p, n in pairs[f] if f in (p, n)][0] for f in range(N)}
+    slot, lander = {}, {}
+    for own, far in ((mine, other), (other, mine)):
+        for u, (p, n) in enumerate(pairs[own[0]]):
+            slot[p] = 2 * u + (0 if own[0] < far[0] else len(own))
+            slot[n] = slot[p] + 1
+            lander[p], lander[n] = pairs[far[0]][u][1], pairs[far[0]][u][0]
+    me = slot[R]
 
-    def bits(dst):
-        return _bits(topo.mask(core, cores[dst]))
+    def eng(src, dst):
+        return _bits(topo.mask(cores[src], cores[dst]))
 
-    def ident_of(dst):
+    def dst_id(dst):
         rid, pid = topo.addr(cores[dst], core)
         return DstId(rid=rid, pnc=pid)
 
-    def xfer(dsts, src, dst_ap, sem, eng):
-        return RemoteDMATransfer(dst_ids=[ident_of(d) for d in dsts], dma_engine_mask=_mask(eng), remote_sem=sem,
-                                 srcs=[src], dsts=[dst_ap for _ in dsts])
+    def xfer(dsts, src, dst_ap, sem, e):
+        return RemoteDMATransfer(dst_ids=[dst_id(d) for d in dsts], dma_engine_mask=sum(1 << b for b in e),
+                                 remote_sem=sem, srcs=[src], dsts=[dst_ap for _ in dsts])
 
     def mapslot(f):
         return T.maps[:, 256 * f:256 * f + 256]
 
     def par(t, h):
         return t[:, 128 * (h % 2):128 * (h % 2) + 128]
-    TH, OL, BK, BM = [T.th0, T.th1], [T.ol0, T.ol1], [T.bk0, T.bk1], [T.bm0, T.bm1]
-    PAK, PAM, PCK, PCM = [T.pak0, T.pak1], [T.pam0, T.pam1], [T.pck0, T.pck1], [T.pcm0, T.pcm1]
     has_map = R >= 1
     from_st = R == N - 1
-
     done = [0]
 
     def load_tab(n):
         for _ in range(n):
             a = done[0] * CH
-            g.sync.dma_start(T.tabs[:, a:a + CH], T.tab[:, a:a + CH]).then_inc(S.tab, 16)
+            sy.dma_start(T.tabs[:, a:a + CH], T.tab[:, a:a + CH]).then_inc(S.tab, 16)
             done[0] += 1
-    if has_map:
-        g.sync.dma_start(T.bpi[:, :], T.bp[:, :]).then_inc(S.bpld, 16)
 
-    if is_front:
-        for x in (0, 1):
-            t = 2 * slot[R] + x
-            g.scalar.dma_start(T.stc[:, x:x + 1], T.st[t:t + 1, :]).then_inc(S.stld, 16)
+    if has_map:
+        sy.dma_start(T.bpi[:, :], T.bp[:, :]).then_inc(S.bpld, 16)
+    sc.dma_start(T.stc[:, 0:1], T.st[me:me + 1, :]).then_inc(S.stld, 16)
     if from_st:
         for q in range(8):
-            g.scalar.dma_start(T.stf[16 * q:16 * q + 16, :], T.st[:, :]).then_inc(S.stfl, 16)
+            sc.dma_start(T.stf[16 * q:16 * q + 16, :], T.st[:, :]).then_inc(S.stfl, 16)
+    load_tab(2)
 
-    v = g.vector
     if has_map:
         v.memset(T.dmat[:, :], 0.0).then_inc(S.msd, 1)
     v.memset(T.ident[:, :], 0.0).then_inc(S.msi, 1)
-    if is_front:
-        v.memset(T.ones[:, :], 1.0).then_inc(S.mso, 1)
+    v.memset(T.ones[:, :], 1.0).then_inc(S.mso, 1)
+    g.iota(T.pi[:, :], [[0, 8]], 0, 1).then_inc(S.gpi, 1)
     if has_map:
+        sel = lambda ap, pat, fill, base, mul: g.affine_select(ap, ap, pat, A.not_equal, fill, base, mul)
         g.wait_ge(S.msd, 1)
-        g.affine_select(T.dmat[:, :], T.dmat[:, :], [[-1, 128]], A.not_equal, 0.5, 0, 1).then_inc(S.gq, 1)
+        sel(T.dmat[:, :], [[-1, 128]], 0.5, 0, 1).then_inc(S.gq, 1)
         g.wait_ge(S.gq, 1)
-        g.affine_select(T.dmat[:, :], T.dmat[:, :], [[1, 128]], A.not_equal, -0.5, -1, -1).then_inc(S.gq, 1)
+        sel(T.dmat[:, :], [[1, 128]], -0.5, -8, -1).then_inc(S.gq, 1)
         g.wait_ge(S.gq, 2)
-        g.affine_select(T.dmat[:, :], T.dmat[:, :], [[-1, 128]], A.not_equal, 0.5, -127, 1).then_inc(S.gdm, 1)
+        sel(T.dmat[:, 1:8], [[-1, 7]], -0.5, -120, 1).then_inc(S.gdm, 1)
+        sel(T.dmat[:, 0:1], [[-1, 1]], 0.5, -127, 1).then_inc(S.gdm, 1)
     g.wait_ge(S.msi, 1)
     g.affine_select(T.ident[:, :], T.ident[:, :], [[-1, 128]], A.not_equal, 1.0, 0, 1).then_inc(S.gid, 1)
-    if is_front:
-        g.iota(T.pcol[:, 0:1], [[1, 1]], 0, 1, allow_small_or_imprecise_dtypes=True).then_inc(S.gpb, 1)
-        g.iota(T.bcol[:, 0:1], [[1, 1]], 1, -2, allow_small_or_imprecise_dtypes=True).then_inc(S.gpb, 1)
-    if not from_st:
-        g.iota(T.du1[:, :], [[0, 8]], 0, 1).then_inc(S.gdu, 1)
-
+    g.iota(T.pcol[:, 0:1], [[1, 1]], 0, 1, allow_small_or_imprecise_dtypes=True).then_inc(S.gpc, 1)
     dv = [0]
 
     def inc(op):
@@ -169,269 +116,197 @@ def rank_program(g, core, T, topo):
 
     def dvw():
         v.wait_ge(S.dv, dv[0])
+    v.wait_ge(S.gpi, 1)
+    inc(v.tensor_scalar(T.p1[:, :], T.pi[:, :], 7, None, A.bitwise_and))
+    inc(v.tensor_scalar(T.p2[:, :], T.pi[:, :], 3, None, A.arith_shift_right))
+    dvw()
+    inc(v.tensor_scalar(T.p3[:, :], T.p1[:, :], -32, 1, A.mult, A.add))
+    inc(v.tensor_scalar(T.p4[:, :], T.p2[:, :], -2, None, A.mult))
+    dvw()
+    v.tensor_tensor(T.bcol[:, 0:1], T.p3[:, 0:1], T.p4[:, 0:1], A.add).then_inc(S.bco, 1)
+
     if has_map:
         v.wait_ge(S.bpld, 16)
-        inc(v.tensor_scalar(T.i1[:, :], T.bpi[:, :], 15, None, A.bitwise_and))
-        inc(v.tensor_scalar(T.i2[:, :], T.bpi[:, :], 11, None, A.arith_shift_right))
-        dvw()
-        inc(v.tensor_scalar(T.i3[:, :], T.i1[:, :], 8, None, A.mult))
+        inc(v.tensor_scalar(T.i1[:, :], T.bpi[:, :], 7, 112, A.arith_shift_right, A.bitwise_and))
+        inc(v.tensor_scalar(T.i2[:, :], T.bpi[:, :], 15, None, A.bitwise_and))
         inc(v.tensor_scalar(T.i4[:, :], T.bpi[:, :], 4, 127, A.arith_shift_right, A.bitwise_and))
         dvw()
-        v.tensor_tensor(T.kd[:, :], T.i3[:, :], T.i2[:, :], A.add).then_inc(S.dkd, 1)
+        v.tensor_tensor(T.kd[:, :], T.i1[:, :], T.i2[:, :], A.add).then_inc(S.dkd, 1)
         v.tensor_copy(T.md[:, :], T.i4[:, :]).then_inc(S.dmd, 1)
-        g.tensor.wait_ge(S.gdm, 1)
-        g.tensor.wait_ge(S.dkd, 1)
-        g.tensor.matmul(T.pak0[:, 0:128], T.dmat[:, :], T.kd[:, :], True, True).then_inc(S.pdk, 1)
-        g.tensor.wait_ge(S.dmd, 1)
-        g.tensor.matmul(T.pam0[:, 0:128], T.dmat[:, :], T.md[:, :], True, True).then_inc(S.pdm, 1)
+        te.wait_ge(S.gdm, 2)
+        te.wait_ge(S.dkd, 1)
+        te.matmul(T.pak[:, 0:128], T.dmat[:, :], T.kd[:, :], True, True).then_inc(S.pdk, 1)
+        te.wait_ge(S.dmd, 1)
+        te.matmul(T.pam[:, 0:128], T.dmat[:, :], T.md[:, :], True, True).then_inc(S.pdm, 1)
         v.wait_ge(S.pdk, 1)
-        v.tensor_copy(T.maps[:, 256 * R:256 * R + 128], T.pak0[:, 0:128]).then_inc(S.mk, 1)
-        g.scalar.wait_ge(S.pdm, 1)
-        g.scalar.activation(T.maps[:, 256 * R + 128:256 * R + 256], T.pam0[:, 0:128], F.Copy).then_inc(S.mm, 1)
-    if not from_st:
-        g.scalar.wait_ge(S.gid, 1)
-        for t, w in ((T.w1, 2048.0), (T.w2, 16.0), (T.w3, -16384.0)):
-            g.scalar.activation(t[:, :], T.ident[:, :], F.Copy, scale=w).then_inc(S.wi, 1)
+        v.tensor_copy(T.maps[:, 256 * R:256 * R + 128], T.pak[:, 0:128]).then_inc(S.mk, 1)
+        sc.wait_ge(S.pdm, 1)
+        sc.activation(T.maps[:, 256 * R + 128:256 * R + 256], T.pam[:, 0:128], F.Copy).then_inc(S.mm, 1)
 
-    def repeat_offsets():
-        v.wait_ge(S.gdu, 1)
-        inc(v.tensor_scalar(T.du2[:, :], T.du1[:, :], 15, None, A.bitwise_and))
-        dvw()
-        v.tensor_copy(T.dur[:, :], T.du2[:, :]).then_inc(S.duo, 1)
-        v.tensor_scalar(T.duk[:, 0:8], T.du2[:, :], 2, None, A.mult).then_inc(S.duo, 1)
-        v.tensor_scalar(T.duk[:, 8:16], T.du2[:, :], 2, 1, A.mult, A.add).then_inc(S.duo, 1)
-    if is_front:
-        v.wait_ge(S.stld, 32)
-        inc(v.tensor_scalar(T.s1[:, :], T.stc[:, :], 15, None, A.bitwise_and))
-        inc(v.tensor_scalar(T.s2[:, :], T.stc[:, :], 11, None, A.arith_shift_right))
-        inc(v.tensor_scalar(T.s4[:, :], T.stc[:, :], 4, 127, A.arith_shift_right, A.bitwise_and))
-        dvw()
-        inc(v.tensor_scalar(T.s3[:, :], T.s1[:, :], 8, None, A.mult))
-        inc(v.tensor_copy(T.d0[:, 2:4], T.s4[:, :]))
-        dvw()
-        inc(v.tensor_tensor(T.d0[:, 0:2], T.s3[:, :], T.s2[:, :], A.add))
-        dvw()
-        v.wait_ge(S.gid, 1)
-        for j in range(4):
-            v.tensor_scalar(T.z[:, 128 * j:128 * j + 128], T.ident[:, :], T.d0[:, j:j + 1], None,
-                            A.mult).then_inc(S.zz, 1)
-        te = g.tensor
-        te.wait_ge(S.mso, 1)
-        te.wait_ge(S.zz, 4)
+    v.wait_ge(S.stld, 16)
+    inc(v.tensor_scalar(T.s1[:, :], T.stc[:, :], 7, 112, A.arith_shift_right, A.bitwise_and))
+    inc(v.tensor_scalar(T.s2[:, :], T.stc[:, :], 15, None, A.bitwise_and))
+    inc(v.tensor_scalar(T.s4[:, :], T.stc[:, :], 4, 127, A.arith_shift_right, A.bitwise_and))
+    dvw()
+    inc(v.tensor_tensor(T.d0[:, 0:1], T.s1[:, :], T.s2[:, :], A.add))
+    inc(v.tensor_copy(T.d0[:, 1:2], T.s4[:, :]))
+    dvw()
+    v.wait_ge(S.gid, 1)
+    for j in (0, 1):
+        v.tensor_scalar(T.z[:, 128 * j:128 * j + 128], T.ident[:, :], T.d0[:, j:j + 1], None, A.mult).then_inc(S.zz, 1)
+    te.wait_ge(S.mso, 1)
+    te.wait_ge(S.zz, 2)
+    if has_map:
         te.wait_ge(S.mk, 1)
         te.wait_ge(S.mm, 1)
-        for x in (0, 1):
-            te.matmul(PCK[x][:, 0:128], T.ones[:, :], T.z[:, 128 * x:128 * x + 128], True, True).then_inc(S["ck%d" % x], 1)
-            te.matmul(PCM[x][:, 0:128], T.ones[:, :], T.z[:, 256 + 128 * x:384 + 128 * x], True,
-                      True).then_inc(S["cm%d" % x], 1)
-        v.wait_ge(S.gpb, 2)
-        g.scalar.wait_ge(S.gpb, 2)
-        if from_st:
-            v.wait_ge(S.stfl, 128)
-            v.tensor_copy(T.off[:, :], T.stf[:, :]).then_inc(S.of, 1)
-    if not from_st:
-        repeat_offsets()
+    te.matmul(T.pck[:, 0:128], T.ones[:, :], T.z[:, 0:128], True, True).then_inc(S.ck, 1)
+    te.matmul(T.pcm[:, 0:128], T.ones[:, :], T.z[:, 128:256], True, True).then_inc(S.cm, 1)
+    v.wait_ge(S.gpc, 1)
+    sc.wait_ge(S.bco, 1)
 
-    if is_front:
-        me = slot[R]
+    def code(h):
+        sc.wait_ge(S.ck, h + 1)
+        sc.activation(par(T.th, h), T.pck[:, 0:128], F.Sign, bias=T.bcol[:, 0:1], scale=2.0).then_inc(S.th, 1)
+        v.wait_ge(S.cm, h + 1)
+        v.tensor_scalar(par(T.ol, h), T.pcm[:, 0:128], T.pcol[:, 0:1], None, A.is_equal).then_inc(S.ol, 1)
 
-        def code(x, h):
-            g.scalar.wait_ge(S["ck%d" % x], h + 1)
-            g.scalar.activation(par(TH[x], h), PCK[x][:, 0:128], F.Sign, bias=T.bcol[:, 0:1],
-                                scale=2.0).then_inc(S["th%d" % x], 1)
-            v.wait_ge(S["cm%d" % x], h + 1)
-            v.tensor_scalar(par(OL[x], h), PCM[x][:, 0:128], T.pcol[:, 0:1], None,
-                            A.is_equal).then_inc(S["ol%d" % x], 1)
+    def results(h):
+        f = HOPS - 1 - h
+        pr = (T.pr0, T.pr1)[h % 2]
+        if h > 1:
+            te.wait_ge(S.ev, h - 1)
+        te.matmul(pr[:, 0:2], par(T.bk, h), T.ones[:, 0:2], True, True)
+        te.matmul(pr[:, 2:4], par(T.bm, h), T.ones[:, 0:2], True, True).then_inc(S.cr, 1)
+        out = T.colall[:, 4 * me:4 * me + 4] if f == R else T.dd[:, 8 * f:8 * f + 4]
+        v.wait_ge(S.cr, h + 1)
+        v.tensor_copy(out, pr[:, 0:4]).then_inc(S.ev, 1)
 
-        def evac(x, h):
-            f = HOPS - 1 - h
-            out = T.colall[:, 4 * me + 2 * x:4 * me + 2 * x + 2] if f == R else T.dd[:, 8 * f + 2 * x:8 * f + 2 * x + 2]
-            v.wait_ge(S["cm%d" % x], h + 2)
-            v.tensor_copy(out, PCM[x][:, 128:130]).then_inc(S["ev%d" % x], 1)
+    code(0)
+    if from_st:
+        v.wait_ge(S.stfl, 128)
+        v.tensor_copy(T.off[:, :], T.stf[:, :]).then_inc(S.of, 1)
+    else:
+        sc.wait_ge(S.gid, 1)
+        for t, w in ((T.w1, 2032.0), (T.w2, 16.0)):
+            sc.activation(t[:, :], T.ident[:, :], F.Copy, scale=w).then_inc(S.wi, 1)
+        inc(v.tensor_scalar(T.p5[:, :], T.pi[:, :], 15, None, A.bitwise_and))
+        dvw()
+        v.tensor_copy(T.duc[:, :], T.p5[:, :]).then_inc(S.duo, 1)
+        v.tensor_scalar(T.duk[:, 0:8], T.p5[:, :], 4, None, A.mult).then_inc(S.duo, 1)
+        v.tensor_scalar(T.duk[:, 8:16], T.p5[:, :], 4, 2, A.mult, A.add).then_inc(S.duo, 1)
+    for h in range(HOPS):
+        f, last = N - 1 - h, h == HOPS - 1
+        te.wait_ge(S.th, h + 1)
+        if f != R:
+            te.wait_ge(S["map%d" % f], len(eng(port[f], R)) if f in other and lander[f] == R else len(eng(R, partner[R])))
+        te.matmul(T.pak[:, 0:128], T.maps[:, 256 * f:256 * f + 128], par(T.th, h), True, True).then_inc(S.ak, 1)
+        te.matmul(T.pam[:, 0:128], T.maps[:, 256 * f + 128:256 * f + 256], par(T.th, h), True, True).then_inc(S.am, 1)
+        v.wait_ge(S.ol, h + 1)
+        v.wait_ge(S.ak, h + 1)
+        v.tensor_tensor(par(T.bk, h), T.pak[:, 0:128], par(T.ol, h), A.mult).then_inc(S.bk, 1)
+        v.wait_ge(S.am, h + 1)
+        v.tensor_tensor(par(T.bm, h), T.pam[:, 0:128], par(T.ol, h), A.mult).then_inc(S.bm, 1)
+        if h:
+            results(h - 1)
+        te.wait_ge(S.bk, h + 1)
+        if not last:
+            te.matmul(T.pck[:, 0:128], T.ones[:, :], par(T.bk, h), True, True).then_inc(S.ck, 1)
+        te.wait_ge(S.bm, h + 1)
+        if not last:
+            te.matmul(T.pcm[:, 0:128], T.ones[:, :], par(T.bm, h), True, True).then_inc(S.cm, 1)
+            code(h + 1)
+    results(HOPS - 1)
 
-        def rows(x, h):
-            f = N - 1 - h
-            te.wait_ge(S["th%d" % x], h + 1)
-            if x == 0 and f != R:
-                if f in front:
-                    n = len(bits(f))
-                elif lander[f] == R:
-                    n = len(_bits(topo.mask(cores[back[0]], core) or topo.mask(core, cores[back[0]]) or
-                                  topo.mask(cores[bpairs[0][0]], core)))
-                else:
-                    n = len(bits(lander[f]))
-                te.wait_ge(S["map%d" % f], n)
-            te.matmul(PAK[x][:, 0:128], T.maps[:, 256 * f:256 * f + 128], par(TH[x], h), True,
-                      True).then_inc(S["ak%d" % x], 1)
-            te.matmul(PAM[x][:, 0:128], T.maps[:, 256 * f + 128:256 * f + 256], par(TH[x], h), True,
-                      True).then_inc(S["am%d" % x], 1)
-
-        def pick(x, h):
-            v.wait_ge(S["ol%d" % x], h + 1)
-            v.wait_ge(S["ak%d" % x], h + 1)
-            v.tensor_tensor(par(BK[x], h), PAK[x][:, 0:128], par(OL[x], h), A.mult).then_inc(S["bk%d" % x], 1)
-            v.wait_ge(S["am%d" % x], h + 1)
-            v.tensor_tensor(par(BM[x], h), PAM[x][:, 0:128], par(OL[x], h), A.mult).then_inc(S["bm%d" % x], 1)
-
-        def sums(x, h):
-            last = h == HOPS - 1
-            te.wait_ge(S["bk%d" % x], h + 1)
-            if not last:
-                te.matmul(PCK[x][:, 0:128], T.ones[:, :], par(BK[x], h), True, True).then_inc(S["ck%d" % x], 1)
-            te.wait_ge(S["bm%d" % x], h + 1)
-            if h:
-                te.wait_ge(S["ev%d" % x], h)
-            if not last:
-                te.matmul(PCM[x][:, 0:128], T.ones[:, :], par(BM[x], h), True, True)
-            te.matmul(PCM[x][:, 128:129], par(BK[x], h), T.ones[:, 0:1], True, True)
-            te.matmul(PCM[x][:, 129:130], par(BM[x], h), T.ones[:, 0:1], True, True).then_inc(S["cm%d" % x], 1)
-
-        code(0, 0)
-        code(1, 0)
-        for h in range(HOPS):
-            rows(0, h)
-            pick(0, h)
-            if h:
-                sums(1, h - 1)
-                code(1, h)
-                evac(1, h - 1)
-            rows(1, h)
-            pick(1, h)
-            sums(0, h)
-            if h < HOPS - 1:
-                code(0, h + 1)
-            evac(0, h)
-        sums(1, HOPS - 1)
-        evac(1, HOPS - 1)
-
-    nsent = [0]
-    relay_map = None
+    nsent, nb, nl, ne = 0, 0, 0, 0
+    peers = [mine[(mine.index(R) + k) % len(mine)] for k in range(1, len(mine))]
+    peers.sort(key=lambda f: (R == port[R] or f != port[R], f == port[f]))
+    home = eng(R, peers[0])
     if has_map:
         g.wait_ge(S.mk, 1)
         g.wait_ge(S.mm, 1)
-    if is_front:
-        peers = [front[(front.index(R) + k) % len(front)] for k in range(1, len(front))]
-        eng = bits(peers[0])
-        g.remote_dma_fused([xfer(peers, mapslot(R), mapslot(R), S["map%d" % R], eng)], local_sem=S.bsent)
-        nb = len(eng)
-        landed = [f for f in back if lander[f] == R and f >= 1]
-        for f in landed:
-            src = [p for p, n in bpairs if f in (p, n)][0]
-            g.wait_ge(S["map%d" % f], len(_bits(topo.mask(cores[src], core))))
-            g.remote_dma_fused([xfer(peers, mapslot(f), mapslot(f), S["map%d" % f], eng)], local_sem=S.sent)
-            nsent[0] += nb
-        port = [p for p, n in fpairs if R in (p, n)][0]
-        mate = [n for p, n in fpairs if p == port][0]
-        ne = 0
-        for k, fs in enumerate(BATCHES):
-            urgent = fs == [0]
-            to_front = fs[0] in front
-            todo = [f for f in fs if f != R]
-            g.wait_ge(S.ev0, HOPS - fs[-1])
-            g.wait_ge(S.ev1, HOPS - fs[-1])
-            if to_front:
-                dst, w = (lambda f: f), 4
-                out = T.colall[:, 4 * me:4 * me + 4]
-            elif R == port:
-                inb = _bits(topo.mask(cores[mate], core))
-                per = len(inb) if urgent else len(inb) // 4
-                g.wait_ge(S["rel%d" % k], per * len(fs))
-                dst, w = (lambda f: f), 8
-                out = T.colall[:, 4 * me:4 * me + 8]
+        g.remote_dma_fused([xfer(peers, mapslot(R), mapslot(R), S["map%d" % R], home)], local_sem=S.bsent)
+        nb = len(home)
+    if R == port[R]:
+        for f in (R, partner[R]):
+            if f >= 1:
+                away = eng(R, lander[f])
+                if f != R:
+                    g.wait_ge(S["map%d" % f], len(eng(f, R)))
+                g.remote_dma_fused([xfer([lander[f]], mapslot(f), mapslot(f), S["map%d" % f], away)], local_sem=S.sent)
+                nsent += len(away)
+    for f in other:
+        if lander[f] == R and f >= 1:
+            g.wait_ge(S["map%d" % f], len(eng(port[f], R)))
+            g.remote_dma_fused([xfer(peers, mapslot(f), mapslot(f), S["map%d" % f], home)], local_sem=S.lsent)
+            nl = len(home)
+    for k, fs in enumerate(BATCHES):
+        urgent = fs == [0]
+        if [f for f in fs if f != R]:
+            g.wait_ge(S.ev, HOPS - fs[-1])
+        relayed = fs[0] in other and R == port[R]
+        if relayed:
+            e = eng(partner[R], R)
+            g.wait_ge(S["rel%d" % k], len(e) if urgent else len(e) // 4 * len(fs))
+        trs = []
+        for j, f in enumerate([f for f in fs if f != R]):
+            to = f if fs[0] in mine or relayed else port[R]
+            e = eng(R, to)
+            if not urgent:
+                e = e[len(e) // 4 * j:len(e) // 4 * (j + 1)]
+            if to == f:
+                out, sem = T.colall[:, 4 * me:4 * me + (8 if relayed else 4)], S.col
             else:
-                dst, w = (lambda f: port), 4
-                out = None
-            trs = []
-            for j, f in enumerate(todo):
-                e = bits(dst(f))
-                if not urgent:
-                    q = len(e) // 4
-                    e = e[q * j:q * j + q]
-                o = out if out is not None else T.dd[:, 8 * f + 4:8 * f + 8]
-                sem = S["rel%d" % k] if out is None else S.col
-                trs.append(xfer([dst(f)], T.dd[:, 8 * f:8 * f + w], o, sem, e))
-                if urgent:
-                    ne = len(e)
-                else:
-                    nsent[0] += len(e)
+                out, sem = T.dd[:, 8 * f + 4:8 * f + 8], S["rel%d" % k]
+            trs.append(xfer([to], T.dd[:, 8 * f:8 * f + (8 if relayed else 4)], out, sem, e))
+            ne, nsent = (len(e), nsent) if urgent else (ne, nsent + len(e))
+        if trs:
             g.remote_dma_fused(trs, local_sem=S.esent if urgent else S.sent)
-    elif has_map:
-        port = [p for p, n in bpairs if R in (p, n)][0]
-        mate = [n for p, n in bpairs if p == port][0]
-        to = lander[R] if R == port else port
-        e = bits(to)
-        g.remote_dma_fused([xfer([to], mapslot(R), mapslot(R), S["map%d" % R], e)], local_sem=S.bsent)
-        nb = len(e)
-        if R == port and mate >= 1:
-            relay_map = mate
-            g.wait_ge(S["map%d" % mate], len(_bits(topo.mask(cores[mate], core))))
-            e = bits(lander[mate])
-            g.remote_dma_fused([xfer([lander[mate]], mapslot(mate), mapslot(mate), S["map%d" % mate], e)],
-                               local_sem=S.fsent)
-            nf = len(e)
+    g.wait_ge(S.sent, nsent)
+    if ne:
+        g.wait_ge(S.esent, ne)
 
-    if is_front:
-        if not from_st:
-            load_tab(1)
-        g.sync.wait_ge(S.bsent, nb)
-        load_tab(3)
-        for h in range(9):
-            g.sync.wait_ge(S.ev0, h + 1)
-            load_tab(1)
-        g.sync.wait_ge(S.esent, ne)
-        load_tab(NCH - done[0])
-        if nsent[0]:
-            g.wait_ge(S.sent, nsent[0])
-    elif has_map:
-        load_tab(2)
-        g.sync.wait_ge(S.bsent, nb)
-        if relay_map is not None:
-            load_tab(3)
-            g.sync.wait_ge(S.fsent, nf)
-        load_tab(NCH - done[0])
-    else:
-        load_tab(NCH)
+    if has_map:
+        sy.wait_ge(S.bsent, nb)
+    load_tab(1)
+    if nl:
+        sy.wait_ge(S.lsent, nl)
+    load_tab(1)
+    for h in TAB_AT:
+        sy.wait_ge(S.ev, h + 1)
+        load_tab(1)
 
     if not from_st:
-        if is_front:
-            total = (len(front) - 1) * (len(bits(peers[0])) // 4)
-        else:
-            per = len(_bits(topo.mask(cores[fpairs[0][0]], core)))
-            total = len(fpairs) * (per if R == 0 else per // 4)
-        for q in (v, g.scalar):
+        h4 = 1 if R == 0 else 4
+        total = (len(mine) - 1) * (len(home) // h4) + len(pairs[other[0]]) * (len(eng(port[other[0]], R)) // h4)
+        for q in (v, sc):
             q.wait_ge(S.col, total)
-            if is_front:
-                q.wait_ge(S.ev0, HOPS)
-                q.wait_ge(S.ev1, HOPS)
+            q.wait_ge(S.ev, HOPS)
             q.wait_ge(S.duo, 3)
-        v.tensor_scalar(T.ri[:, :], T.colall[:, 0:32:2], 0.125, -0.4375, A.mult, A.add).then_inc(S.rr, 1)
+        v.tensor_scalar(T.ci[:, :], T.colall[:, 0:64:4], 0.0625, -0.46875, A.mult, A.add).then_inc(S.rr, 1)
         v.wait_ge(S.rr, 1)
-        v.tensor_copy(T.ltr[:, :], T.ri[:, 0:16].indirect(T.dur[:, 0:8])).then_inc(S.lr, 1)
-        g.scalar.activation(T.ltk[:, :], T.colall[:, 0:32].indirect(T.duk[:, 0:16]), F.Copy).then_inc(S.lk, 1)
-        te = g.tensor
-        te.wait_ge(S.wi, 3)
-        te.wait_ge(S.gid, 1)
-        te.wait_ge(S.lr, 1)
-        po = T.pck0[:, 0:128]
-        te.matmul(po, T.ltr[:, :], T.w3[:, :], True, False)
-        te.matmul(po, T.ltr[:, :], T.ident[:, :], False, False)
+        v.tensor_copy(T.ltc[:, :], T.ci[:, 0:16].indirect(T.duc[:, 0:8])).then_inc(S.lc, 1)
+        sc.activation(T.ltk[:, :], T.colall[:, 0:64].indirect(T.duk[:, 0:16]), F.Copy).then_inc(S.lk, 1)
+        te.wait_ge(S.wi, 2)
+        te.wait_ge(S.lc, 1)
+        po = T.pof[:, 0:128]
+        te.matmul(po, T.ltc[:, :], T.w1[:, :], True, False)
         te.wait_ge(S.lk, 1)
-        te.matmul(po, T.ltk[:, 0:128], T.w1[:, :], False, False)
+        te.matmul(po, T.ltk[:, 0:128], T.ident[:, :], False, False)
         te.matmul(po, T.ltk[:, 128:256], T.w2[:, :], False, True).then_inc(S.po, 1)
         v.wait_ge(S.po, 1)
         v.tensor_copy(T.off[:, :], po).then_inc(S.of, 1)
 
-    for q, base, names in ((v, 0, ("yv0", "yv1")), (g.scalar, 1024, ("ya0", "ya1"))):
+    pieces = [("yv0", v, 0, 640), ("ya0", sc, 1024, 640), ("yv1", v, 640, 384), ("ya1", sc, 1664, 384)]
+    for q in (v, sc):
         q.wait_ge(S.of, 1)
         q.wait_ge(S.tab, 16 * NCH)
-        for k, nm in enumerate(names):
-            a = base + 512 * k
-            src = T.tabs[:, 0:16384].indirect(T.off[:, a // 16:a // 16 + 32])
-            if base:
-                q.activation(T.yt[:, a:a + 512], src, F.Copy).then_inc(S[nm], 1)
-            else:
-                q.tensor_copy(T.yt[:, a:a + 512], src).then_inc(S[nm], 1)
-    for a, nm in ((0, "yv0"), (1024, "ya0"), (512, "yv1"), (1536, "ya1")):
-        g.sync.wait_ge(S[nm], 1)
-        g.sync.dma_start(T.y[:, a:a + 512], T.yt[:, a:a + 512]).then_inc(S.yst, 16)
-    g.sync.wait_ge(S.yst, 64)
+    for nm, q, a, n in pieces:
+        src = T.tabs[:, 0:16384].indirect(T.off[:, a // 16:(a + n) // 16])
+        if q is sc:
+            q.activation(T.yt[:, a:a + n], src, F.Copy).then_inc(S[nm], 1)
+        else:
+            q.tensor_copy(T.yt[:, a:a + n], src).then_inc(S[nm], 1)
+    for nm, q, a, n in pieces:
+        sy.wait_ge(S[nm], 1)
+        sy.dma_start(T.y[:, a:a + n], T.yt[:, a:a + n]).then_inc(S.yst, 16)
+    sy.wait_ge(S.yst, 64)

@@ -2,25 +2,28 @@ from concourse.bass import DstId, RemoteDMATransfer
 from concourse.mybir import AluOpType, ActivationFunctionType
 
 N = 16
+WORLD = 256
 CH = 2048
 NCH = 16384 // CH
 HOPS = N - 1
 BATCHES = [[14, 13, 12, 11], [10, 9, 8], [7, 6, 5, 4], [3, 2, 1], [0]]
-TAB_AT = (1, 3, 5, 7)
+TAB_AT = (0, 1, 2, 4, 6, 8)
 
 SCRATCH = {}
 for _dt, _names in (("bfloat16", "tabs:16384 yt:2048 maps:4096 kd:128 md:128 dmat:128 ident:128 ones:128 w1:128 w2:128 "
                                  "z:256 th:256 ol:256 bk:256 bm:256 ltc:128 ltk:256"),
-                    ("int32", "bpi:128 i1:128 i2:128 i4:128 stc:1 s1:1 s2:1 s4:1 stf:128 pi:8 p1:8 p2:8 p3:8 p4:8 p5:8 "
-                              "ci:16"),
+                    ("int32", "bpi:128 i1:128 i2:128 i4:128 stx:2 sts:2 s1:1 s2:1 s4:1 stf:128 pi:8 p1:8 p2:8 p3:8 "
+                              "p4:8 p5:8 ci:16"),
                     ("float32", "pcol:4 bcol:4 d0:2 dd:128 colall:64"),
                     ("uint16", "duc:8 duk:16 off:128")):
     for _e in _names.split():
         SCRATCH[_e.split(":")[0]] = ("sbuf", [128, int(_e.split(":")[1])], _dt)
-for _e in ("pak", "pam", "pck", "pcm", "pr0", "pr1", "pof"):
-    SCRATCH[_e] = ("psum", [128, 512], "float32")
-SEMAPHORES = ("bpld stld stfl tab yst msd msi mso gq gdm gid gpc gpi bco dv dkd dmd pdk pdm mk mm zz wi duo bsent lsent "
-              "sent esent col th ol ak am bk bm ck cm cr ev rr lc lk po of yv0 yv1 ya0 ya1").split()
+for _e in ("pak", "pam", "pck", "pcm"):
+    for _s in "01":
+        SCRATCH[_e + _s] = ("psum", [128, 512], "float32")
+SEMAPHORES = ("bpld stld stsl stfl tab yst msd msi mso gq gdm gid gpc gpi bco dv dkd dmd pdk pdm mk mm zz wi duo bsent "
+              "lsent sent stsent esent col cr ev rr lc lk po of yv0 yv1 ya0 ya1").split()
+SEMAPHORES += [n + s for n in "th ol ak am bk bm ck cm".split() for s in "01"]
 SEMAPHORES += ["map%d" % f for f in range(1, N)] + ["rel%d" % k for k in range(len(BATCHES))]
 
 
@@ -29,39 +32,47 @@ def _bits(mask):
 
 
 def rank_program(g, core, T, topo):
-    R = T.rank_of(core)
-    if R is None:
+    cores = list(T.cores)
+    place = lambda c: (topo.host(c), topo.chip(c))
+    NEAR = [c for c in cores if place(c) == place(cores[0])]
+    FAR = [c for c in cores if place(c) == place(cores[N - 1])]
+    HELP = [c for c in range(WORLD) if c not in cores and topo.mates(c, cores[N - 1]) and topo.same_plane(c, cores[0])]
+    if core not in NEAR + FAR + HELP:
         return
+    R = T.rank_of(core)
     A, F, S = AluOpType, ActivationFunctionType, T.sem
     v, te, sc, sy = g.vector, g.tensor, g.scalar, g.sync
-    cores = list(T.cores)
-    place = lambda f: (topo.host(cores[f]), topo.chip(cores[f]))
-    mine = [f for f in range(N) if place(f) == place(R)]
-    other = [f for f in range(N) if f not in mine]
+    chain = core not in FAR
+    helper = core in HELP
+    mine = NEAR if core in NEAR else FAR if core in FAR else HELP
+    rank = {c: f for f, c in enumerate(cores)}
+    far_maps = [rank[c] for c in FAR]
 
     def pair_up(own, far):
         out = []
-        for d in sorted(set(topo.die(cores[f]) for f in own)):
-            on = [f for f in own if topo.die(cores[f]) == d]
-            ports = [f for f in on if topo.may_write(cores[f], cores[far])]
-            out += list(zip(ports, [f for f in on if f not in ports]))
+        for d in sorted(set(topo.die(c) for c in own)):
+            on = [c for c in own if topo.die(c) == d]
+            ports = [c for c in on if topo.may_write(c, far)]
+            out += list(zip(ports, [c for c in on if c not in ports]))
         return out
-    pairs = {f: pair_up(own, far[0]) for own, far in ((mine, other), (other, mine)) for f in own}
-    port = {f: [p for p, n in pairs[f] if f in (p, n)][0] for f in range(N)}
-    partner = {f: [n + p - f for p, n in pairs[f] if f in (p, n)][0] for f in range(N)}
-    slot, lander = {}, {}
-    for own, far in ((mine, other), (other, mine)):
-        for u, (p, n) in enumerate(pairs[own[0]]):
-            slot[p] = 2 * u + (0 if own[0] < far[0] else len(own))
-            slot[n] = slot[p] + 1
-            lander[p], lander[n] = pairs[far[0]][u][1], pairs[far[0]][u][0]
-    me = slot[R]
+    port, partner, slot = {}, {}, {}
+    for own, far, base in ((NEAR, FAR[0], 0), (HELP, FAR[0], len(NEAR)), (FAR, NEAR[0], None)):
+        for u, (p, n) in enumerate(pair_up(own, far)):
+            port[p] = port[n] = p
+            partner[p], partner[n] = n, p
+            if base is not None:
+                slot[p], slot[n] = base + 2 * u, base + 2 * u + 1
+    land_near = {f: NEAR[(N - 1 - f) % len(NEAR)] for f in far_maps}
+    land_help = {f: HELP[(N - 1 - f) % len(HELP)] for f in range(1, N)}
+    fports = sorted([c for c in FAR if port[c] == c], reverse=True)
+    st_from = dict(zip(fports + NEAR[:2], HELP[:len(fports) + 2]))
+    st_pass = dict(zip(HELP, [c for c in reversed(HELP) if c not in st_from.values()]))
 
     def eng(src, dst):
-        return _bits(topo.mask(cores[src], cores[dst]))
+        return _bits(topo.mask(src, dst))
 
     def dst_id(dst):
-        rid, pid = topo.addr(cores[dst], core)
+        rid, pid = topo.addr(dst, core)
         return DstId(rid=rid, pnc=pid)
 
     def xfer(dsts, src, dst_ap, sem, e):
@@ -71,9 +82,13 @@ def rank_program(g, core, T, topo):
     def mapslot(f):
         return T.maps[:, 256 * f:256 * f + 256]
 
-    def par(t, h):
+    def part(t, h, s):
+        a = 128 * (h % 2) + 64 * s
+        return t[:, a:a + 64]
+
+    def full(t, h):
         return t[:, 128 * (h % 2):128 * (h % 2) + 128]
-    has_map = R >= 1
+    has_map = R is not None and R >= 1
     from_st = R == N - 1
     done = [0]
 
@@ -85,18 +100,26 @@ def rank_program(g, core, T, topo):
 
     if has_map:
         sy.dma_start(T.bpi[:, :], T.bp[:, :]).then_inc(S.bpld, 16)
-    sc.dma_start(T.stc[:, 0:1], T.st[me:me + 1, :]).then_inc(S.stld, 16)
+    nsts = 0
+    if core in st_from:
+        to = st_from[core]
+        for k, h in enumerate([to] + ([st_pass[to]] if to in st_pass else [])):
+            sc.dma_start(T.sts[:, k:k + 1], T.st[slot[h]:slot[h] + 1, :]).then_inc(S.stsl, 16)
+            nsts += 1
+    if chain and not helper:
+        sc.dma_start(T.stx[:, 0:1], T.st[slot[core]:slot[core] + 1, :]).then_inc(S.stld, 16)
     if from_st:
         for q in range(8):
             sc.dma_start(T.stf[16 * q:16 * q + 16, :], T.st[:, :]).then_inc(S.stfl, 16)
-    load_tab(2)
 
-    if has_map:
-        v.memset(T.dmat[:, :], 0.0).then_inc(S.msd, 1)
-    v.memset(T.ident[:, :], 0.0).then_inc(S.msi, 1)
-    v.memset(T.ones[:, :], 1.0).then_inc(S.mso, 1)
-    g.iota(T.pi[:, :], [[0, 8]], 0, 1).then_inc(S.gpi, 1)
-    if has_map:
+    def small_constants():
+        g.iota(T.pi[:, :], [[0, 8]], 0, 1).then_inc(S.gpi, 1)
+        if chain:
+            g.iota(T.pcol[:, 0:1], [[1, 1]], 0, 1, allow_small_or_imprecise_dtypes=True).then_inc(S.gpc, 1)
+        g.wait_ge(S.msi, 1)
+        g.affine_select(T.ident[:, :], T.ident[:, :], [[-1, 128]], A.not_equal, 1.0, 0, 1).then_inc(S.gid, 1)
+
+    def difference_matrix():
         sel = lambda ap, pat, fill, base, mul: g.affine_select(ap, ap, pat, A.not_equal, fill, base, mul)
         g.wait_ge(S.msd, 1)
         sel(T.dmat[:, :], [[-1, 128]], 0.5, 0, 1).then_inc(S.gq, 1)
@@ -105,194 +128,303 @@ def rank_program(g, core, T, topo):
         g.wait_ge(S.gq, 2)
         sel(T.dmat[:, 1:8], [[-1, 7]], -0.5, -120, 1).then_inc(S.gdm, 1)
         sel(T.dmat[:, 0:1], [[-1, 1]], 0.5, -127, 1).then_inc(S.gdm, 1)
-    g.wait_ge(S.msi, 1)
-    g.affine_select(T.ident[:, :], T.ident[:, :], [[-1, 128]], A.not_equal, 1.0, 0, 1).then_inc(S.gid, 1)
-    g.iota(T.pcol[:, 0:1], [[1, 1]], 0, 1, allow_small_or_imprecise_dtypes=True).then_inc(S.gpc, 1)
+
+    def send_st():
+        to = st_from[core]
+        e = eng(core, to)
+        g.wait_ge(S.stsl, 16 * nsts)
+        g.remote_dma_fused([xfer([to], T.sts[:, 0:nsts], T.stx[:, 0:nsts], S.stld, e)], local_sem=S.stsent)
+        return len(e)
+    nsent, nss = 0, 0
+    if chain:
+        v.memset(T.ident[:, :], 0.0).then_inc(S.msi, 1)
+        v.memset(T.ones[:, :], 1.0).then_inc(S.mso, 1)
+        if has_map:
+            v.memset(T.dmat[:, :], 0.0).then_inc(S.msd, 1)
+        small_constants()
+        if nsts:
+            nss = send_st()
+        if has_map:
+            difference_matrix()
+    else:
+        v.memset(T.dmat[:, :], 0.0).then_inc(S.msd, 1)
+        if not from_st:
+            v.memset(T.ident[:, :], 0.0).then_inc(S.msi, 1)
+        difference_matrix()
+        if nsts:
+            nss = send_st()
     dv = [0]
 
     def inc(op):
         op.then_inc(S.dv, 1)
         dv[0] += 1
 
-    def dvw():
-        v.wait_ge(S.dv, dv[0])
-    v.wait_ge(S.gpi, 1)
-    inc(v.tensor_scalar(T.p1[:, :], T.pi[:, :], 7, None, A.bitwise_and))
-    inc(v.tensor_scalar(T.p2[:, :], T.pi[:, :], 3, None, A.arith_shift_right))
-    dvw()
-    inc(v.tensor_scalar(T.p3[:, :], T.p1[:, :], -32, 1, A.mult, A.add))
-    inc(v.tensor_scalar(T.p4[:, :], T.p2[:, :], -2, None, A.mult))
-    dvw()
-    v.tensor_tensor(T.bcol[:, 0:1], T.p3[:, 0:1], T.p4[:, 0:1], A.add).then_inc(S.bco, 1)
+    def dvw(back=0):
+        v.wait_ge(S.dv, dv[0] - back)
 
-    if has_map:
+    def prepare_map():
         v.wait_ge(S.bpld, 16)
-        inc(v.tensor_scalar(T.i1[:, :], T.bpi[:, :], 7, 112, A.arith_shift_right, A.bitwise_and))
-        inc(v.tensor_scalar(T.i2[:, :], T.bpi[:, :], 15, None, A.bitwise_and))
-        inc(v.tensor_scalar(T.i4[:, :], T.bpi[:, :], 4, 127, A.arith_shift_right, A.bitwise_and))
+        if R == 1:
+            inc(v.tensor_scalar(T.i1[:, :], T.bpi[:, :], 7, None, A.arith_shift_right))
+            inc(v.tensor_scalar(T.i4[:, :], T.bpi[:, :], 127, None, A.bitwise_and))
+            dvw(1)
+            v.tensor_copy(T.kd[:, :], T.i1[:, :]).then_inc(S.dkd, 1)
+        else:
+            inc(v.tensor_scalar(T.i1[:, :], T.bpi[:, :], 7, 112, A.arith_shift_right, A.bitwise_and))
+            inc(v.tensor_scalar(T.i2[:, :], T.bpi[:, :], 15, None, A.bitwise_and))
+            inc(v.tensor_scalar(T.i4[:, :], T.bpi[:, :], 4, 127, A.arith_shift_right, A.bitwise_and))
+            dvw(1)
+            v.tensor_tensor(T.kd[:, :], T.i1[:, :], T.i2[:, :], A.add).then_inc(S.dkd, 1)
         dvw()
-        v.tensor_tensor(T.kd[:, :], T.i1[:, :], T.i2[:, :], A.add).then_inc(S.dkd, 1)
         v.tensor_copy(T.md[:, :], T.i4[:, :]).then_inc(S.dmd, 1)
         te.wait_ge(S.gdm, 2)
         te.wait_ge(S.dkd, 1)
-        te.matmul(T.pak[:, 0:128], T.dmat[:, :], T.kd[:, :], True, True).then_inc(S.pdk, 1)
+        te.matmul(T.pak0[:, 0:128], T.dmat[:, :], T.kd[:, :], True, True).then_inc(S.pdk, 1)
         te.wait_ge(S.dmd, 1)
-        te.matmul(T.pam[:, 0:128], T.dmat[:, :], T.md[:, :], True, True).then_inc(S.pdm, 1)
+        te.matmul(T.pam0[:, 0:128], T.dmat[:, :], T.md[:, :], True, True).then_inc(S.pdm, 1)
         v.wait_ge(S.pdk, 1)
-        v.tensor_copy(T.maps[:, 256 * R:256 * R + 128], T.pak[:, 0:128]).then_inc(S.mk, 1)
+        v.tensor_copy(T.maps[:, 256 * R:256 * R + 128], T.pak0[:, 0:128]).then_inc(S.mk, 1)
         sc.wait_ge(S.pdm, 1)
-        sc.activation(T.maps[:, 256 * R + 128:256 * R + 256], T.pam[:, 0:128], F.Copy).then_inc(S.mm, 1)
+        sc.activation(T.maps[:, 256 * R + 128:256 * R + 256], T.pam0[:, 0:128], F.Copy).then_inc(S.mm, 1)
 
-    v.wait_ge(S.stld, 16)
-    inc(v.tensor_scalar(T.s1[:, :], T.stc[:, :], 7, 112, A.arith_shift_right, A.bitwise_and))
-    inc(v.tensor_scalar(T.s2[:, :], T.stc[:, :], 15, None, A.bitwise_and))
-    inc(v.tensor_scalar(T.s4[:, :], T.stc[:, :], 4, 127, A.arith_shift_right, A.bitwise_and))
-    dvw()
-    inc(v.tensor_tensor(T.d0[:, 0:1], T.s1[:, :], T.s2[:, :], A.add))
-    inc(v.tensor_copy(T.d0[:, 1:2], T.s4[:, :]))
-    dvw()
-    v.wait_ge(S.gid, 1)
-    for j in (0, 1):
-        v.tensor_scalar(T.z[:, 128 * j:128 * j + 128], T.ident[:, :], T.d0[:, j:j + 1], None, A.mult).then_inc(S.zz, 1)
-    te.wait_ge(S.mso, 1)
-    te.wait_ge(S.zz, 2)
-    if has_map:
-        te.wait_ge(S.mk, 1)
-        te.wait_ge(S.mm, 1)
-    te.matmul(T.pck[:, 0:128], T.ones[:, :], T.z[:, 0:128], True, True).then_inc(S.ck, 1)
-    te.matmul(T.pcm[:, 0:128], T.ones[:, :], T.z[:, 128:256], True, True).then_inc(S.cm, 1)
-    v.wait_ge(S.gpc, 1)
-    sc.wait_ge(S.bco, 1)
-
-    def code(h):
-        sc.wait_ge(S.ck, h + 1)
-        sc.activation(par(T.th, h), T.pck[:, 0:128], F.Sign, bias=T.bcol[:, 0:1], scale=2.0).then_inc(S.th, 1)
-        v.wait_ge(S.cm, h + 1)
-        v.tensor_scalar(par(T.ol, h), T.pcm[:, 0:128], T.pcol[:, 0:1], None, A.is_equal).then_inc(S.ol, 1)
-
-    def results(h):
-        f = HOPS - 1 - h
-        pr = (T.pr0, T.pr1)[h % 2]
-        if h > 1:
-            te.wait_ge(S.ev, h - 1)
-        te.matmul(pr[:, 0:2], par(T.bk, h), T.ones[:, 0:2], True, True)
-        te.matmul(pr[:, 2:4], par(T.bm, h), T.ones[:, 0:2], True, True).then_inc(S.cr, 1)
-        out = T.colall[:, 4 * me:4 * me + 4] if f == R else T.dd[:, 8 * f:8 * f + 4]
-        v.wait_ge(S.cr, h + 1)
-        v.tensor_copy(out, pr[:, 0:4]).then_inc(S.ev, 1)
-
-    code(0)
-    if from_st:
-        v.wait_ge(S.stfl, 128)
-        v.tensor_copy(T.off[:, :], T.stf[:, :]).then_inc(S.of, 1)
-    else:
+    def tail_constants():
         sc.wait_ge(S.gid, 1)
-        for t, w in ((T.w1, 2032.0), (T.w2, 16.0)):
+        for t, w in ((T.w1, 128.0 if R == 0 else 2032.0), (T.w2, 16.0)):
             sc.activation(t[:, :], T.ident[:, :], F.Copy, scale=w).then_inc(S.wi, 1)
+        v.wait_ge(S.gpi, 1)
         inc(v.tensor_scalar(T.p5[:, :], T.pi[:, :], 15, None, A.bitwise_and))
         dvw()
         v.tensor_copy(T.duc[:, :], T.p5[:, :]).then_inc(S.duo, 1)
         v.tensor_scalar(T.duk[:, 0:8], T.p5[:, :], 4, None, A.mult).then_inc(S.duo, 1)
         v.tensor_scalar(T.duk[:, 8:16], T.p5[:, :], 4, 2, A.mult, A.add).then_inc(S.duo, 1)
-    for h in range(HOPS):
-        f, last = N - 1 - h, h == HOPS - 1
-        te.wait_ge(S.th, h + 1)
-        if f != R:
-            te.wait_ge(S["map%d" % f], len(eng(port[f], R)) if f in other and lander[f] == R else len(eng(R, partner[R])))
-        te.matmul(T.pak[:, 0:128], T.maps[:, 256 * f:256 * f + 128], par(T.th, h), True, True).then_inc(S.ak, 1)
-        te.matmul(T.pam[:, 0:128], T.maps[:, 256 * f + 128:256 * f + 256], par(T.th, h), True, True).then_inc(S.am, 1)
-        v.wait_ge(S.ol, h + 1)
-        v.wait_ge(S.ak, h + 1)
-        v.tensor_tensor(par(T.bk, h), T.pak[:, 0:128], par(T.ol, h), A.mult).then_inc(S.bk, 1)
-        v.wait_ge(S.am, h + 1)
-        v.tensor_tensor(par(T.bm, h), T.pam[:, 0:128], par(T.ol, h), A.mult).then_inc(S.bm, 1)
-        if h:
-            results(h - 1)
-        te.wait_ge(S.bk, h + 1)
-        if not last:
-            te.matmul(T.pck[:, 0:128], T.ones[:, :], par(T.bk, h), True, True).then_inc(S.ck, 1)
-        te.wait_ge(S.bm, h + 1)
-        if not last:
-            te.matmul(T.pcm[:, 0:128], T.ones[:, :], par(T.bm, h), True, True).then_inc(S.cm, 1)
-            code(h + 1)
-    results(HOPS - 1)
 
-    nsent, nb, nl, ne = 0, 0, 0, 0
-    peers = [mine[(mine.index(R) + k) % len(mine)] for k in range(1, len(mine))]
-    peers.sort(key=lambda f: (R == port[R] or f != port[R], f == port[f]))
-    home = eng(R, peers[0])
-    if has_map:
+    if not chain:
+        prepare_map()
+        if from_st:
+            v.wait_ge(S.stfl, 128)
+            v.tensor_copy(T.off[:, :], T.stf[:, :]).then_inc(S.of, 1)
+        else:
+            tail_constants()
+    else:
+        v.wait_ge(S.gpi, 1)
+        inc(v.tensor_scalar(T.p1[:, :], T.pi[:, :], 7, None, A.bitwise_and))
+        inc(v.tensor_scalar(T.p2[:, :], T.pi[:, :], 3, None, A.arith_shift_right))
+        dvw()
+        inc(v.tensor_scalar(T.p3[:, :], T.p1[:, :], -32, 1, A.mult, A.add))
+        inc(v.tensor_scalar(T.p4[:, :], T.p2[:, :], -2, None, A.mult))
+        dvw()
+        v.tensor_tensor(T.bcol[:, 0:1], T.p3[:, 0:1], T.p4[:, 0:1], A.add).then_inc(S.bco, 1)
+
+        if helper:
+            src = [c for c in st_from if st_from[c] == core] or [c for c in st_pass if st_pass[c] == core]
+            nst = len(eng(src[0], core))
+        else:
+            nst = 16
+        v.wait_ge(S.stld, nst)
+        row = T.stx[:, 0:1]
+        inc(v.tensor_scalar(T.s1[:, :], row, 7, 112, A.arith_shift_right, A.bitwise_and))
+        inc(v.tensor_scalar(T.s2[:, :], row, 15, None, A.bitwise_and))
+        inc(v.tensor_scalar(T.s4[:, :], row, 4, 127, A.arith_shift_right, A.bitwise_and))
+        dvw()
+        inc(v.tensor_tensor(T.d0[:, 0:1], T.s1[:, :], T.s2[:, :], A.add))
+        inc(v.tensor_copy(T.d0[:, 1:2], T.s4[:, :]))
+        dvw()
+        v.wait_ge(S.gid, 1)
+        for j in (0, 1):
+            v.tensor_scalar(T.z[:, 128 * j:128 * j + 128], T.ident[:, :], T.d0[:, j:j + 1], None,
+                            A.mult).then_inc(S.zz, 1)
+        te.wait_ge(S.mso, 1)
+        te.wait_ge(S.zz, 2)
+        for s in (0, 1):
+            for j, nm in ((0, "ck"), (1, "cm")):
+                a = 128 * j + 64 * s
+                te.matmul(T["p%s%d" % (nm, s)][:, 0:64], T.ones[:, :], T.z[:, a:a + 64], True,
+                          True).then_inc(S["%s%d" % (nm, s)], 1)
+        if has_map:
+            prepare_map()
+            te.wait_ge(S.mk, 1)
+            te.wait_ge(S.mm, 1)
+        v.wait_ge(S.gpc, 1)
+        sc.wait_ge(S.bco, 1)
+
+        def code(h):
+            for s in (0, 1):
+                sc.wait_ge(S["ck%d" % s], h + 1)
+                sc.activation(part(T.th, h, s), T["pck%d" % s][:, 0:64], F.Sign, bias=T.bcol[:, 0:1],
+                              scale=2.0).then_inc(S["th%d" % s], 1)
+            for s in (0, 1):
+                v.wait_ge(S["cm%d" % s], h + 1)
+                v.tensor_scalar(part(T.ol, h, s), T["pcm%d" % s][:, 0:64], T.pcol[:, 0:1], None,
+                                A.is_equal).then_inc(S["ol%d" % s], 1)
+
+        def results(h):
+            f = HOPS - 1 - h
+            te.wait_ge(S.ol1, min(h + 2, HOPS))
+            if h:
+                te.wait_ge(S.ev, h)
+            te.matmul(T.pcm1[:, 128:130], full(T.bk, h), T.ones[:, 0:2], True, True)
+            te.matmul(T.pcm1[:, 130:132], full(T.bm, h), T.ones[:, 0:2], True, True).then_inc(S.cr, 1)
+            out = T.colall[:, 4 * slot[core]:4 * slot[core] + 4] if f == R else T.dd[:, 8 * f:8 * f + 4]
+            sc.wait_ge(S.cr, h + 1)
+            sc.activation(out, T.pcm1[:, 128:132], F.Copy).then_inc(S.ev, 1)
+
+        code(0)
+        if not helper:
+            tail_constants()
+        for h in range(HOPS):
+            f, last = N - 1 - h, h == HOPS - 1
+            if f != R:
+                land = land_help if helper else land_near
+                if f in far_maps:
+                    frm = port[cores[f]] if land[f] == core else land[f]
+                else:
+                    frm = cores[f] if not helper or land[f] == core else land[f]
+                te.wait_ge(S["map%d" % f], len(eng(frm, core)))
+            for s in (0, 1):
+                te.wait_ge(S["th%d" % s], h + 1)
+                for j, nm in ((0, "ak"), (1, "am")):
+                    a = 256 * f + 128 * j
+                    te.matmul(T["p%s%d" % (nm, s)][:, 0:64], T.maps[:, a:a + 128], part(T.th, h, s), True,
+                              True).then_inc(S["%s%d" % (nm, s)], 1)
+            for s in (0, 1):
+                v.wait_ge(S["ol%d" % s], h + 1)
+                for nm, out in (("k", T.bk), ("m", T.bm)):
+                    v.wait_ge(S["a%s%d" % (nm, s)], h + 1)
+                    v.tensor_tensor(part(out, h, s), T["pa%s%d" % (nm, s)][:, 0:64], part(T.ol, h, s),
+                                    A.mult).then_inc(S["b%s%d" % (nm, s)], 1)
+            if h:
+                results(h - 1)
+            for s in (0, 1):
+                for nm, src in (("k", T.bk), ("m", T.bm)):
+                    te.wait_ge(S["b%s%d" % (nm, s)], h + 1)
+                    if not last:
+                        if h and nm == "m" and s == 1:
+                            te.wait_ge(S.ev, h)
+                        te.matmul(T["pc%s%d" % (nm, s)][:, 0:64], T.ones[:, :], part(src, h, s), True,
+                                  True).then_inc(S["c%s%d" % (nm, s)], 1)
+            if not last:
+                code(h + 1)
+        results(HOPS - 1)
+
+    nb, nl, ne = 0, 0, 0
+    peers = [mine[(mine.index(core) + k) % len(mine)] for k in range(1, len(mine))]
+    home = eng(core, peers[0])
+    if not chain:
+        ports = [R, rank[partner[core]]] if port[core] == core else []
         g.wait_ge(S.mk, 1)
         g.wait_ge(S.mm, 1)
-        g.remote_dma_fused([xfer(peers, mapslot(R), mapslot(R), S["map%d" % R], home)], local_sem=S.bsent)
-        nb = len(home)
-    if R == port[R]:
-        for f in (R, partner[R]):
-            if f >= 1:
-                away = eng(R, lander[f])
-                if f != R:
-                    g.wait_ge(S["map%d" % f], len(eng(f, R)))
-                g.remote_dma_fused([xfer([lander[f]], mapslot(f), mapslot(f), S["map%d" % f], away)], local_sem=S.sent)
-                nsent += len(away)
-    for f in other:
-        if lander[f] == R and f >= 1:
-            g.wait_ge(S["map%d" % f], len(eng(port[f], R)))
-            g.remote_dma_fused([xfer(peers, mapslot(f), mapslot(f), S["map%d" % f], home)], local_sem=S.lsent)
-            nl = len(home)
-    for k, fs in enumerate(BATCHES):
+        if not ports:
+            p = port[core]
+            g.remote_dma_fused([xfer([p], mapslot(R), mapslot(R), S["map%d" % R], eng(core, p))], local_sem=S.sent)
+            nsent += len(eng(core, p))
+        for f in ports:
+            if f != R:
+                g.wait_ge(S["map%d" % f], len(eng(cores[f], core)))
+            e = eng(core, land_near[f])
+            g.remote_dma_fused([xfer([land_near[f], land_help[f]], mapslot(f), mapslot(f), S["map%d" % f], e)],
+                               local_sem=S.sent)
+            nsent += len(e)
+        if not from_st:
+            small_constants()
+    else:
+        if core in st_pass:
+            g.wait_ge(S.stld, nst)
+            to = st_pass[core]
+            g.remote_dma_fused([xfer([to], T.stx[:, 1:2], T.stx[:, 0:1], S.stld, home)], local_sem=S.sent)
+            nsent += len(home)
+        land = land_help if helper else land_near
+        for f in sorted(land, reverse=True):
+            if land[f] == core:
+                g.wait_ge(S["map%d" % f], len(eng(port[cores[f]] if f in far_maps else cores[f], core)))
+                g.remote_dma_fused([xfer(peers, mapslot(f), mapslot(f), S["map%d" % f], home)], local_sem=S.lsent)
+                nl += len(home)
+        if has_map:
+            g.wait_ge(S.mk, 1)
+            g.wait_ge(S.mm, 1)
+            g.remote_dma_fused([xfer(peers, mapslot(R), mapslot(R), S["map%d" % R], home)], local_sem=S.bsent)
+            e = eng(core, land_help[R])
+            g.remote_dma_fused([xfer([land_help[R]], mapslot(R), mapslot(R), S["map%d" % R], e)], local_sem=S.bsent)
+            nb = len(home) + len(e)
+
+    for k, fs in enumerate(BATCHES if chain else []):
         urgent = fs == [0]
-        if [f for f in fs if f != R]:
-            g.wait_ge(S.ev, HOPS - fs[-1])
-        relayed = fs[0] in other and R == port[R]
-        if relayed:
-            e = eng(partner[R], R)
+        todo = [f for f in fs if f != R]
+        if not todo:
+            continue
+        g.wait_ge(S.ev, HOPS - fs[-1])
+        direct = all(topo.may_write(c, cores[fs[0]]) for c in mine if c != cores[fs[0]])
+        both = not direct and port[core] == core
+        if both:
+            e = eng(partner[core], core)
             g.wait_ge(S["rel%d" % k], len(e) if urgent else len(e) // 4 * len(fs))
         trs = []
-        for j, f in enumerate([f for f in fs if f != R]):
-            to = f if fs[0] in mine or relayed else port[R]
-            e = eng(R, to)
+        for j, f in enumerate(todo):
+            to = cores[f] if direct or both else port[core]
+            e = eng(core, to)
             if not urgent:
                 e = e[len(e) // 4 * j:len(e) // 4 * (j + 1)]
-            if to == f:
-                out, sem = T.colall[:, 4 * me:4 * me + (8 if relayed else 4)], S.col
+            w = 8 if both else 4
+            if to == cores[f]:
+                out, sem = T.colall[:, 4 * slot[core]:4 * slot[core] + w], S.col
             else:
                 out, sem = T.dd[:, 8 * f + 4:8 * f + 8], S["rel%d" % k]
-            trs.append(xfer([to], T.dd[:, 8 * f:8 * f + (8 if relayed else 4)], out, sem, e))
+            trs.append(xfer([to], T.dd[:, 8 * f:8 * f + w], out, sem, e))
             ne, nsent = (len(e), nsent) if urgent else (ne, nsent + len(e))
-        if trs:
-            g.remote_dma_fused(trs, local_sem=S.esent if urgent else S.sent)
+        g.remote_dma_fused(trs, local_sem=S.esent if urgent else S.sent)
     g.wait_ge(S.sent, nsent)
+    if nss:
+        g.wait_ge(S.stsent, nss)
     if ne:
         g.wait_ge(S.esent, ne)
+    if helper:
+        if nl:
+            g.wait_ge(S.lsent, nl)
+        return
 
-    if has_map:
-        sy.wait_ge(S.bsent, nb)
-    load_tab(1)
-    if nl:
-        sy.wait_ge(S.lsent, nl)
-    load_tab(1)
-    for h in TAB_AT:
-        sy.wait_ge(S.ev, h + 1)
+    if chain:
+        if nss:
+            sy.wait_ge(S.stsent, nss)
         load_tab(1)
+        if nl:
+            sy.wait_ge(S.lsent, nl)
+        if nb:
+            sy.wait_ge(S.bsent, nb)
+        load_tab(1)
+        for h in TAB_AT:
+            sy.wait_ge(S.ev, h + 1)
+            load_tab(1)
+    else:
+        sy.wait_ge(S.sent, nsent)
+        load_tab(NCH)
 
     if not from_st:
         h4 = 1 if R == 0 else 4
-        total = (len(mine) - 1) * (len(home) // h4) + len(pairs[other[0]]) * (len(eng(port[other[0]], R)) // h4)
+        senders = [c for c in NEAR + HELP if c != core and (chain or port[c] == c)]
+        total = sum(len(eng(c, core)) // h4 for c in senders)
         for q in (v, sc):
             q.wait_ge(S.col, total)
-            q.wait_ge(S.ev, HOPS)
+            if chain:
+                q.wait_ge(S.ev, HOPS)
             q.wait_ge(S.duo, 3)
-        v.tensor_scalar(T.ci[:, :], T.colall[:, 0:64:4], 0.0625, -0.46875, A.mult, A.add).then_inc(S.rr, 1)
-        v.wait_ge(S.rr, 1)
-        v.tensor_copy(T.ltc[:, :], T.ci[:, 0:16].indirect(T.duc[:, 0:8])).then_inc(S.lc, 1)
-        sc.activation(T.ltk[:, :], T.colall[:, 0:64].indirect(T.duk[:, 0:16]), F.Copy).then_inc(S.lk, 1)
+        po = T.pck0[:, 0:128]
         te.wait_ge(S.wi, 2)
-        te.wait_ge(S.lc, 1)
-        po = T.pof[:, 0:128]
-        te.matmul(po, T.ltc[:, :], T.w1[:, :], True, False)
-        te.wait_ge(S.lk, 1)
-        te.matmul(po, T.ltk[:, 0:128], T.ident[:, :], False, False)
-        te.matmul(po, T.ltk[:, 128:256], T.w2[:, :], False, True).then_inc(S.po, 1)
+        if R == 0:
+            v.tensor_copy(T.ltc[:, :], T.colall[:, 0:64].indirect(T.duk[:, 0:8])).then_inc(S.lc, 1)
+            sc.activation(T.ltk[:, 0:128], T.colall[:, 0:64].indirect(T.duk[:, 8:16]), F.Copy).then_inc(S.lk, 1)
+            te.wait_ge(S.lc, 1)
+            te.matmul(po, T.ltc[:, :], T.w1[:, :], True, False)
+            te.wait_ge(S.lk, 1)
+            te.matmul(po, T.ltk[:, 0:128], T.ident[:, :], False, True).then_inc(S.po, 1)
+        else:
+            v.tensor_scalar(T.ci[:, :], T.colall[:, 0:64:4], 0.0625, -0.46875, A.mult, A.add).then_inc(S.rr, 1)
+            v.wait_ge(S.rr, 1)
+            v.tensor_copy(T.ltc[:, :], T.ci[:, 0:16].indirect(T.duc[:, 0:8])).then_inc(S.lc, 1)
+            sc.activation(T.ltk[:, :], T.colall[:, 0:64].indirect(T.duk[:, 0:16]), F.Copy).then_inc(S.lk, 1)
+            te.wait_ge(S.lc, 1)
+            te.matmul(po, T.ltc[:, :], T.w1[:, :], True, False)
+            te.wait_ge(S.lk, 1)
+            te.matmul(po, T.ltk[:, 0:128], T.ident[:, :], False, False)
+            te.matmul(po, T.ltk[:, 128:256], T.w2[:, :], False, True).then_inc(S.po, 1)
         v.wait_ge(S.po, 1)
         v.tensor_copy(T.off[:, :], po).then_inc(S.of, 1)
 

from concourse.bass import DstId, RemoteDMATransfer
from concourse.mybir import AluOpType, ActivationFunctionType

N = 16
WORLD = 256
CH = 2048
NCH = 16384 // CH
HOPS = N - 1
BATCHES = [[14, 13, 12, 11], [10, 9, 8], [7, 6, 5, 4], [3, 2, 1], [0]]
TAB_AT = (0, 1, 2, 4, 6, 8)

SCRATCH = {}
for _dt, _names in (("bfloat16", "tabs:16384 yt:2048 maps:4096 kd:128 md:128 dmat:128 ident:128 ones:128 w1:128 w2:128 "
                                 "z:256 th:256 ol:256 bk:256 bm:256 ltc:128 ltk:256"),
                    ("int32", "bpi:128 i1:128 i2:128 i4:128 stx:2 sts:2 s1:1 s2:1 s4:1 stf:128 pi:8 p1:8 p2:8 p3:8 "
                              "p4:8 p5:8 ci:16"),
                    ("float32", "pcol:4 bcol:4 d0:2 dd:128 colall:64"),
                    ("uint16", "duc:8 duk:16 off:128")):
    for _e in _names.split():
        SCRATCH[_e.split(":")[0]] = ("sbuf", [128, int(_e.split(":")[1])], _dt)
for _e in ("pak", "pam", "pck", "pcm"):
    for _s in "01":
        SCRATCH[_e + _s] = ("psum", [128, 512], "float32")
SEMAPHORES = ("bpld stld stsl stfl tab yst msd msi mso gq gdm gid gpc gpi bco dv dkd dmd pdk pdm mk mm zz wi duo bsent "
              "lsent sent stsent esent col cr ev rr lc lk po of yv0 yv1 ya0 ya1").split()
SEMAPHORES += [n + s for n in "th ol ak am bk bm ck cm".split() for s in "01"]
SEMAPHORES += ["map%d" % f for f in range(1, N)] + ["rel%d" % k for k in range(len(BATCHES))]


def _bits(mask):
    return [b for b in range(16) if mask >> b & 1]


def rank_program(g, core, T, topo):
    cores = list(T.cores)
    place = lambda c: (topo.host(c), topo.chip(c))
    NEAR = [c for c in cores if place(c) == place(cores[0])]
    FAR = [c for c in cores if place(c) == place(cores[N - 1])]
    HELP = [c for c in range(WORLD) if c not in cores and topo.mates(c, cores[N - 1]) and topo.same_plane(c, cores[0])]
    if core not in NEAR + FAR + HELP:
        return
    R = T.rank_of(core)
    A, F, S = AluOpType, ActivationFunctionType, T.sem
    v, te, sc, sy = g.vector, g.tensor, g.scalar, g.sync
    chain = core not in FAR
    helper = core in HELP
    mine = NEAR if core in NEAR else FAR if core in FAR else HELP
    rank = {c: f for f, c in enumerate(cores)}
    far_maps = [rank[c] for c in FAR]

    def pair_up(own, far):
        out = []
        for d in sorted(set(topo.die(c) for c in own)):
            on = [c for c in own if topo.die(c) == d]
            ports = [c for c in on if topo.may_write(c, far)]
            out += list(zip(ports, [c for c in on if c not in ports]))
        return out
    port, partner, slot = {}, {}, {}
    for own, far, base in ((NEAR, FAR[0], 0), (HELP, FAR[0], len(NEAR)), (FAR, NEAR[0], None)):
        for u, (p, n) in enumerate(pair_up(own, far)):
            port[p] = port[n] = p
            partner[p], partner[n] = n, p
            if base is not None:
                slot[p], slot[n] = base + 2 * u, base + 2 * u + 1
    land_near = {f: NEAR[(N - 1 - f) % len(NEAR)] for f in far_maps}
    land_help = {f: HELP[(N - 1 - f) % len(HELP)] for f in range(1, N)}
    fports = sorted([c for c in FAR if port[c] == c], reverse=True)
    st_from = dict(zip(fports + NEAR[:2], HELP[:len(fports) + 2]))
    st_pass = dict(zip(HELP, [c for c in reversed(HELP) if c not in st_from.values()]))

    def eng(src, dst):
        return _bits(topo.mask(src, dst))

    def dst_id(dst):
        rid, pid = topo.addr(dst, core)
        return DstId(rid=rid, pnc=pid)

    def xfer(dsts, src, dst_ap, sem, e):
        return RemoteDMATransfer(dst_ids=[dst_id(d) for d in dsts], dma_engine_mask=sum(1 << b for b in e),
                                 remote_sem=sem, srcs=[src], dsts=[dst_ap for _ in dsts])

    def mapslot(f):
        return T.maps[:, 256 * f:256 * f + 256]

    def part(t, h, s):
        a = 128 * (h % 2) + 64 * s
        return t[:, a:a + 64]

    def full(t, h):
        return t[:, 128 * (h % 2):128 * (h % 2) + 128]
    has_map = R is not None and R >= 1
    from_st = R == N - 1
    done = [0]

    def load_tab(n):
        for _ in range(n):
            a = done[0] * CH
            sy.dma_start(T.tabs[:, a:a + CH], T.tab[:, a:a + CH]).then_inc(S.tab, 16)
            done[0] += 1

    if has_map:
        sy.dma_start(T.bpi[:, :], T.bp[:, :]).then_inc(S.bpld, 16)
    nsts = 0
    if core in st_from:
        to = st_from[core]
        for k, h in enumerate([to] + ([st_pass[to]] if to in st_pass else [])):
            sc.dma_start(T.sts[:, k:k + 1], T.st[slot[h]:slot[h] + 1, :]).then_inc(S.stsl, 16)
            nsts += 1
    if chain and not helper:
        sc.dma_start(T.stx[:, 0:1], T.st[slot[core]:slot[core] + 1, :]).then_inc(S.stld, 16)
    if from_st:
        for q in range(8):
            sc.dma_start(T.stf[16 * q:16 * q + 16, :], T.st[:, :]).then_inc(S.stfl, 16)

    def small_constants():
        g.iota(T.pi[:, :], [[0, 8]], 0, 1).then_inc(S.gpi, 1)
        if chain:
            g.iota(T.pcol[:, 0:1], [[1, 1]], 0, 1, allow_small_or_imprecise_dtypes=True).then_inc(S.gpc, 1)
        g.wait_ge(S.msi, 1)
        g.affine_select(T.ident[:, :], T.ident[:, :], [[-1, 128]], A.not_equal, 1.0, 0, 1).then_inc(S.gid, 1)

    def difference_matrix():
        sel = lambda ap, pat, fill, base, mul: g.affine_select(ap, ap, pat, A.not_equal, fill, base, mul)
        g.wait_ge(S.msd, 1)
        sel(T.dmat[:, :], [[-1, 128]], 0.5, 0, 1).then_inc(S.gq, 1)
        g.wait_ge(S.gq, 1)
        sel(T.dmat[:, :], [[1, 128]], -0.5, -8, -1).then_inc(S.gq, 1)
        g.wait_ge(S.gq, 2)
        sel(T.dmat[:, 1:8], [[-1, 7]], -0.5, -120, 1).then_inc(S.gdm, 1)
        sel(T.dmat[:, 0:1], [[-1, 1]], 0.5, -127, 1).then_inc(S.gdm, 1)

    def send_st():
        to = st_from[core]
        e = eng(core, to)
        g.wait_ge(S.stsl, 16 * nsts)
        g.remote_dma_fused([xfer([to], T.sts[:, 0:nsts], T.stx[:, 0:nsts], S.stld, e)], local_sem=S.stsent)
        return len(e)
    nsent, nss = 0, 0
    if chain:
        v.memset(T.ident[:, :], 0.0).then_inc(S.msi, 1)
        v.memset(T.ones[:, :], 1.0).then_inc(S.mso, 1)
        if has_map:
            v.memset(T.dmat[:, :], 0.0).then_inc(S.msd, 1)
        small_constants()
        if nsts:
            nss = send_st()
        if has_map:
            difference_matrix()
    else:
        v.memset(T.dmat[:, :], 0.0).then_inc(S.msd, 1)
        if not from_st:
            v.memset(T.ident[:, :], 0.0).then_inc(S.msi, 1)
        difference_matrix()
        if nsts:
            nss = send_st()
    dv = [0]

    def inc(op):
        op.then_inc(S.dv, 1)
        dv[0] += 1

    def dvw(back=0):
        v.wait_ge(S.dv, dv[0] - back)

    def prepare_map():
        v.wait_ge(S.bpld, 16)
        if R == 1:
            inc(v.tensor_scalar(T.i1[:, :], T.bpi[:, :], 7, None, A.arith_shift_right))
            inc(v.tensor_scalar(T.i4[:, :], T.bpi[:, :], 127, None, A.bitwise_and))
            dvw(1)
            v.tensor_copy(T.kd[:, :], T.i1[:, :]).then_inc(S.dkd, 1)
        else:
            inc(v.tensor_scalar(T.i1[:, :], T.bpi[:, :], 7, 112, A.arith_shift_right, A.bitwise_and))
            inc(v.tensor_scalar(T.i2[:, :], T.bpi[:, :], 15, None, A.bitwise_and))
            inc(v.tensor_scalar(T.i4[:, :], T.bpi[:, :], 4, 127, A.arith_shift_right, A.bitwise_and))
            dvw(1)
            v.tensor_tensor(T.kd[:, :], T.i1[:, :], T.i2[:, :], A.add).then_inc(S.dkd, 1)
        dvw()
        v.tensor_copy(T.md[:, :], T.i4[:, :]).then_inc(S.dmd, 1)
        te.wait_ge(S.gdm, 2)
        te.wait_ge(S.dkd, 1)
        te.matmul(T.pak0[:, 0:128], T.dmat[:, :], T.kd[:, :], True, True).then_inc(S.pdk, 1)
        te.wait_ge(S.dmd, 1)
        te.matmul(T.pam0[:, 0:128], T.dmat[:, :], T.md[:, :], True, True).then_inc(S.pdm, 1)
        v.wait_ge(S.pdk, 1)
        v.tensor_copy(T.maps[:, 256 * R:256 * R + 128], T.pak0[:, 0:128]).then_inc(S.mk, 1)
        sc.wait_ge(S.pdm, 1)
        sc.activation(T.maps[:, 256 * R + 128:256 * R + 256], T.pam0[:, 0:128], F.Copy).then_inc(S.mm, 1)

    def tail_constants():
        sc.wait_ge(S.gid, 1)
        for t, w in ((T.w1, 128.0 if R == 0 else 2032.0), (T.w2, 16.0)):
            sc.activation(t[:, :], T.ident[:, :], F.Copy, scale=w).then_inc(S.wi, 1)
        v.wait_ge(S.gpi, 1)
        inc(v.tensor_scalar(T.p5[:, :], T.pi[:, :], 15, None, A.bitwise_and))
        dvw()
        v.tensor_copy(T.duc[:, :], T.p5[:, :]).then_inc(S.duo, 1)
        v.tensor_scalar(T.duk[:, 0:8], T.p5[:, :], 4, None, A.mult).then_inc(S.duo, 1)
        v.tensor_scalar(T.duk[:, 8:16], T.p5[:, :], 4, 2, A.mult, A.add).then_inc(S.duo, 1)

    if not chain:
        prepare_map()
        if from_st:
            v.wait_ge(S.stfl, 128)
            v.tensor_copy(T.off[:, :], T.stf[:, :]).then_inc(S.of, 1)
        else:
            tail_constants()
    else:
        v.wait_ge(S.gpi, 1)
        inc(v.tensor_scalar(T.p1[:, :], T.pi[:, :], 7, None, A.bitwise_and))
        inc(v.tensor_scalar(T.p2[:, :], T.pi[:, :], 3, None, A.arith_shift_right))
        dvw()
        inc(v.tensor_scalar(T.p3[:, :], T.p1[:, :], -32, 1, A.mult, A.add))
        inc(v.tensor_scalar(T.p4[:, :], T.p2[:, :], -2, None, A.mult))
        dvw()
        v.tensor_tensor(T.bcol[:, 0:1], T.p3[:, 0:1], T.p4[:, 0:1], A.add).then_inc(S.bco, 1)

        if helper:
            src = [c for c in st_from if st_from[c] == core] or [c for c in st_pass if st_pass[c] == core]
            nst = len(eng(src[0], core))
        else:
            nst = 16
        v.wait_ge(S.stld, nst)
        row = T.stx[:, 0:1]
        inc(v.tensor_scalar(T.s1[:, :], row, 7, 112, A.arith_shift_right, A.bitwise_and))
        inc(v.tensor_scalar(T.s2[:, :], row, 15, None, A.bitwise_and))
        inc(v.tensor_scalar(T.s4[:, :], row, 4, 127, A.arith_shift_right, A.bitwise_and))
        dvw()
        inc(v.tensor_tensor(T.d0[:, 0:1], T.s1[:, :], T.s2[:, :], A.add))
        inc(v.tensor_copy(T.d0[:, 1:2], T.s4[:, :]))
        dvw()
        v.wait_ge(S.gid, 1)
        for j in (0, 1):
            v.tensor_scalar(T.z[:, 128 * j:128 * j + 128], T.ident[:, :], T.d0[:, j:j + 1], None,
                            A.mult).then_inc(S.zz, 1)
        te.wait_ge(S.mso, 1)
        te.wait_ge(S.zz, 2)
        for s in (0, 1):
            for j, nm in ((0, "ck"), (1, "cm")):
                a = 128 * j + 64 * s
                te.matmul(T["p%s%d" % (nm, s)][:, 0:64], T.ones[:, :], T.z[:, a:a + 64], True,
                          True).then_inc(S["%s%d" % (nm, s)], 1)
        if has_map:
            prepare_map()
            te.wait_ge(S.mk, 1)
            te.wait_ge(S.mm, 1)
        v.wait_ge(S.gpc, 1)
        sc.wait_ge(S.bco, 1)

        def code(h):
            for s in (0, 1):
                sc.wait_ge(S["ck%d" % s], h + 1)
                sc.activation(part(T.th, h, s), T["pck%d" % s][:, 0:64], F.Sign, bias=T.bcol[:, 0:1],
                              scale=2.0).then_inc(S["th%d" % s], 1)
            for s in (0, 1):
                v.wait_ge(S["cm%d" % s], h + 1)
                v.tensor_scalar(part(T.ol, h, s), T["pcm%d" % s][:, 0:64], T.pcol[:, 0:1], None,
                                A.is_equal).then_inc(S["ol%d" % s], 1)

        def results(h):
            f = HOPS - 1 - h
            te.wait_ge(S.ol1, min(h + 2, HOPS))
            if h:
                te.wait_ge(S.ev, h)
            te.matmul(T.pcm1[:, 128:130], full(T.bk, h), T.ones[:, 0:2], True, True)
            te.matmul(T.pcm1[:, 130:132], full(T.bm, h), T.ones[:, 0:2], True, True).then_inc(S.cr, 1)
            out = T.colall[:, 4 * slot[core]:4 * slot[core] + 4] if f == R else T.dd[:, 8 * f:8 * f + 4]
            sc.wait_ge(S.cr, h + 1)
            sc.activation(out, T.pcm1[:, 128:132], F.Copy).then_inc(S.ev, 1)

        code(0)
        if not helper:
            tail_constants()
        for h in range(HOPS):
            f, last = N - 1 - h, h == HOPS - 1
            if f != R:
                land = land_help if helper else land_near
                if f in far_maps:
                    frm = port[cores[f]] if land[f] == core else land[f]
                else:
                    frm = cores[f] if not helper or land[f] == core else land[f]
                te.wait_ge(S["map%d" % f], len(eng(frm, core)))
            for s in (0, 1):
                te.wait_ge(S["th%d" % s], h + 1)
                for j, nm in ((0, "ak"), (1, "am")):
                    a = 256 * f + 128 * j
                    te.matmul(T["p%s%d" % (nm, s)][:, 0:64], T.maps[:, a:a + 128], part(T.th, h, s), True,
                              True).then_inc(S["%s%d" % (nm, s)], 1)
            for s in (0, 1):
                v.wait_ge(S["ol%d" % s], h + 1)
                for nm, out in (("k", T.bk), ("m", T.bm)):
                    v.wait_ge(S["a%s%d" % (nm, s)], h + 1)
                    v.tensor_tensor(part(out, h, s), T["pa%s%d" % (nm, s)][:, 0:64], part(T.ol, h, s),
                                    A.mult).then_inc(S["b%s%d" % (nm, s)], 1)
            if h:
                results(h - 1)
            for s in (0, 1):
                for nm, src in (("k", T.bk), ("m", T.bm)):
                    te.wait_ge(S["b%s%d" % (nm, s)], h + 1)
                    if not last:
                        if h and nm == "m" and s == 1:
                            te.wait_ge(S.ev, h)
                        te.matmul(T["pc%s%d" % (nm, s)][:, 0:64], T.ones[:, :], part(src, h, s), True,
                                  True).then_inc(S["c%s%d" % (nm, s)], 1)
            if not last:
                code(h + 1)
        results(HOPS - 1)

    nb, nl, ne = 0, 0, 0
    peers = [mine[(mine.index(core) + k) % len(mine)] for k in range(1, len(mine))]
    home = eng(core, peers[0])
    if not chain:
        ports = [R, rank[partner[core]]] if port[core] == core else []
        g.wait_ge(S.mk, 1)
        g.wait_ge(S.mm, 1)
        if not ports:
            p = port[core]
            g.remote_dma_fused([xfer([p], mapslot(R), mapslot(R), S["map%d" % R], eng(core, p))], local_sem=S.sent)
            nsent += len(eng(core, p))
        for f in ports:
            if f != R:
                g.wait_ge(S["map%d" % f], len(eng(cores[f], core)))
            e = eng(core, land_near[f])
            g.remote_dma_fused([xfer([land_near[f], land_help[f]], mapslot(f), mapslot(f), S["map%d" % f], e)],
                               local_sem=S.sent)
            nsent += len(e)
        if not from_st:
            small_constants()
    else:
        if core in st_pass:
            g.wait_ge(S.stld, nst)
            to = st_pass[core]
            g.remote_dma_fused([xfer([to], T.stx[:, 1:2], T.stx[:, 0:1], S.stld, home)], local_sem=S.sent)
            nsent += len(home)
        land = land_help if helper else land_near
        for f in sorted(land, reverse=True):
            if land[f] == core:
                g.wait_ge(S["map%d" % f], len(eng(port[cores[f]] if f in far_maps else cores[f], core)))
                g.remote_dma_fused([xfer(peers, mapslot(f), mapslot(f), S["map%d" % f], home)], local_sem=S.lsent)
                nl += len(home)
        if has_map:
            g.wait_ge(S.mk, 1)
            g.wait_ge(S.mm, 1)
            g.remote_dma_fused([xfer(peers, mapslot(R), mapslot(R), S["map%d" % R], home)], local_sem=S.bsent)
            e = eng(core, land_help[R])
            g.remote_dma_fused([xfer([land_help[R]], mapslot(R), mapslot(R), S["map%d" % R], e)], local_sem=S.bsent)
            nb = len(home) + len(e)

    for k, fs in enumerate(BATCHES if chain else []):
        urgent = fs == [0]
        todo = [f for f in fs if f != R]
        if not todo:
            continue
        g.wait_ge(S.ev, HOPS - fs[-1])
        direct = all(topo.may_write(c, cores[fs[0]]) for c in mine if c != cores[fs[0]])
        both = not direct and port[core] == core
        if both:
            e = eng(partner[core], core)
            g.wait_ge(S["rel%d" % k], len(e) if urgent else len(e) // 4 * len(fs))
        trs = []
        for j, f in enumerate(todo):
            to = cores[f] if direct or both else port[core]
            e = eng(core, to)
            if not urgent:
                e = e[len(e) // 4 * j:len(e) // 4 * (j + 1)]
            w = 8 if both else 4
            if to == cores[f]:
                out, sem = T.colall[:, 4 * slot[core]:4 * slot[core] + w], S.col
            else:
                out, sem = T.dd[:, 8 * f + 4:8 * f + 8], S["rel%d" % k]
            trs.append(xfer([to], T.dd[:, 8 * f:8 * f + w], out, sem, e))
            ne, nsent = (len(e), nsent) if urgent else (ne, nsent + len(e))
        g.remote_dma_fused(trs, local_sem=S.esent if urgent else S.sent)
    g.wait_ge(S.sent, nsent)
    if nss:
        g.wait_ge(S.stsent, nss)
    if ne:
        g.wait_ge(S.esent, ne)
    if helper:
        if nl:
            g.wait_ge(S.lsent, nl)
        return

    if chain:
        if nss:
            sy.wait_ge(S.stsent, nss)
        load_tab(1)
        if nl:
            sy.wait_ge(S.lsent, nl)
        if nb:
            sy.wait_ge(S.bsent, nb)
        load_tab(1)
        for h in TAB_AT:
            sy.wait_ge(S.ev, h + 1)
            load_tab(1)
    else:
        sy.wait_ge(S.sent, nsent)
        load_tab(NCH)

    if not from_st:
        h4 = 1 if R == 0 else 4
        senders = [c for c in NEAR + HELP if c != core and (chain or port[c] == c)]
        total = sum(len(eng(c, core)) // h4 for c in senders)
        for q in (v, sc):
            q.wait_ge(S.col, total)
            if chain:
                q.wait_ge(S.ev, HOPS)
            q.wait_ge(S.duo, 3)
        po = T.pck0[:, 0:128]
        te.wait_ge(S.wi, 2)
        if R == 0:
            v.tensor_copy(T.ltc[:, :], T.colall[:, 0:64].indirect(T.duk[:, 0:8])).then_inc(S.lc, 1)
            sc.activation(T.ltk[:, 0:128], T.colall[:, 0:64].indirect(T.duk[:, 8:16]), F.Copy).then_inc(S.lk, 1)
            te.wait_ge(S.lc, 1)
            te.matmul(po, T.ltc[:, :], T.w1[:, :], True, False)
            te.wait_ge(S.lk, 1)
            te.matmul(po, T.ltk[:, 0:128], T.ident[:, :], False, True).then_inc(S.po, 1)
        else:
            v.tensor_scalar(T.ci[:, :], T.colall[:, 0:64:4], 0.0625, -0.46875, A.mult, A.add).then_inc(S.rr, 1)
            v.wait_ge(S.rr, 1)
            v.tensor_copy(T.ltc[:, :], T.ci[:, 0:16].indirect(T.duc[:, 0:8])).then_inc(S.lc, 1)
            sc.activation(T.ltk[:, :], T.colall[:, 0:64].indirect(T.duk[:, 0:16]), F.Copy).then_inc(S.lk, 1)
            te.wait_ge(S.lc, 1)
            te.matmul(po, T.ltc[:, :], T.w1[:, :], True, False)
            te.wait_ge(S.lk, 1)
            te.matmul(po, T.ltk[:, 0:128], T.ident[:, :], False, False)
            te.matmul(po, T.ltk[:, 128:256], T.w2[:, :], False, True).then_inc(S.po, 1)
        v.wait_ge(S.po, 1)
        v.tensor_copy(T.off[:, :], po).then_inc(S.of, 1)

    pieces = [("yv0", v, 0, 640), ("ya0", sc, 1024, 640), ("yv1", v, 640, 384), ("ya1", sc, 1664, 384)]
    for q in (v, sc):
        q.wait_ge(S.of, 1)
        q.wait_ge(S.tab, 16 * NCH)
    for nm, q, a, n in pieces:
        src = T.tabs[:, 0:16384].indirect(T.off[:, a // 16:(a + n) // 16])
        if q is sc:
            q.activation(T.yt[:, a:a + n], src, F.Copy).then_inc(S[nm], 1)
        else:
            q.tensor_copy(T.yt[:, a:a + n], src).then_inc(S[nm], 1)
    for nm, q, a, n in pieces:
        sy.wait_ge(S[nm], 1)
        sy.dma_start(T.y[:, a:a + n], T.yt[:, a:a + n]).then_inc(S.yst, 16)
    sy.wait_ge(S.yst, 64)
